import numpy as np
import ml_dtypes


def mxq(x, axis, fmt="e4m3"):
    dtype, down = {"e4m3": (ml_dtypes.float8_e4m3fn, 7), "e5m2": (ml_dtypes.float8_e5m2, 14)}[fmt]
    v = np.moveaxis(np.asarray(x, np.float32).astype(ml_dtypes.bfloat16).astype(np.float64), axis, -1)
    blocks = v.reshape(v.shape[:-1] + (-1, 32))
    amax = np.abs(blocks).max(-1, keepdims=True)
    byte = np.maximum(np.where(amax > 0, np.frexp(amax)[1] - 1 + 127, 0) - down, 1)
    scale = np.exp2(byte - 127.0)
    codes = (blocks / scale).astype(np.float32).astype(dtype).astype(np.float64)
    return np.moveaxis((codes * scale).reshape(v.shape), -1, axis)


WIDE = False


def mx_kscale(k):
    if not WIDE:
        return np.ones(k)
    levels = np.array([10, -10, 5, -5, 0])
    if k % 512:
        return np.exp2(np.random.permutation(np.resize(levels, k // 32))).repeat(32)
    a = np.empty((k // 512, 16))
    for p in range(k // 512):
        a[p, :8] = np.random.permutation(np.resize(levels, 8))
        for g in range(8):
            far = levels[np.abs(levels - a[p, g]) >= 10]
            a[p, g + 8] = far[np.random.randint(len(far))]
    return np.exp2(a.ravel()).repeat(32)


BF16 = ml_dtypes.bfloat16


def bf(x):
    return np.asarray(x, np.float32).astype(BF16)


def f64(x):
    return np.asarray(x).astype(np.float64)


E2M1 = np.array([0.0, 0.5, 1.0, 1.5, 2.0, 3.0, 4.0, 6.0, -0.0, -0.5, -1.0, -1.5, -2.0, -3.0, -4.0, -6.0])


def pack_weight(w, fmt):
    k, n = w.shape
    w = f64(bf(w)).reshape(k // 32, 32, n)
    amax = np.abs(w).max(1)
    if fmt == "e4m3":
        byte = np.frexp(amax)[1] - 1 + 127 - 7
    else:
        mant, ex = np.frexp(amax / 6.0)
        byte = np.where(mant > 0.5, ex, ex - 1) + 127
    byte = np.clip(np.where(amax > 0, byte, 1), 1, 254)
    scaled = (w * np.exp2(127.0 - byte)[:, None, :]).reshape(k, n).astype(np.float32)
    by_word = np.ascontiguousarray(scaled.reshape(k // 512, 128, 4, n).transpose(0, 1, 3, 2))
    if fmt == "e4m3":
        words = by_word.astype(ml_dtypes.float8_e4m3fn).view(np.uint8)
    else:
        c = by_word.astype(ml_dtypes.float4_e2m1fn).view(np.uint8) & 0xF
        words = c[..., 0::2] | (c[..., 1::2] << 4)
    return np.ascontiguousarray(words), np.ascontiguousarray(byte.astype(np.uint8).reshape(k // 512, 16, n))


def unpack_weight(words, scales, fmt):
    g, p, n, _ = words.shape
    if fmt == "e4m3":
        vals = np.ascontiguousarray(words).view(ml_dtypes.float8_e4m3fn).astype(np.float64)
    else:
        nib = np.empty((g, p, n, 4), np.uint8)
        nib[..., 0::2] = words & 0xF
        nib[..., 1::2] = words >> 4
        vals = E2M1[nib]
    vals = vals * np.repeat(np.exp2(scales.astype(np.float64) - 127.0), 8, axis=1)[..., None]
    return vals.transpose(0, 1, 3, 2).reshape(g * 512, n)
def pack4(w):
    words, scales = pack_weight(w, "e2m1")
    return words.reshape(words.shape[0], 128, -1), scales


def unpack4(words, scales):
    return unpack_weight(words.reshape(words.shape[0], 128, -1, 2), scales, "e2m1")


E4M3FN = np.array([(-1.0 if i & 128 else 1.0) * ((1.0 + (i & 7) / 8.0) * 2.0 ** (((i >> 3) & 15) - 7) if i & 120 else (i & 7) * 2.0 ** -9) for i in range(256)])


def e4m3fn_bytes(y):
    return np.clip(np.asarray(y, np.float64), -448.0, 448.0).astype(np.float32).astype(ml_dtypes.float8_e4m3fn).view(np.uint8)


def e4m3fn_values(b):
    return E4M3FN[b]


N, D, F = 1024, 512, 512
F3 = 3 * F


def draw0():
    s, u = mx_kscale(D), mx_kscale(N)
    x = np.random.standard_normal((N, D)) * s
    w = np.random.standard_normal((D, F3)) / np.sqrt(D) / s[:, None]
    adj = np.random.standard_normal((N, N)) / np.sqrt(N) / u[None, :]
    src_scale = np.random.uniform(0.5, 1.5, N) * u
    mix = 1.5 * np.random.standard_normal((3, F)) / np.sqrt(F)
    words, scales = pack4(w)
    return {"x": bf(x), "w_words": words, "w_scales": scales, "adj": bf(adj), "src_scale": bf(src_scale), "mix": bf(mix)}


def softmax(v):
    e = np.exp(v - v.max(axis=1, keepdims=True))
    return e / e.sum(axis=1, keepdims=True)


def core(x, w_words, w_scales, adj, src_scale, mix):
    x, adj, src_scale, mix = f64(x), f64(adj), f64(src_scale), f64(mix)
    f = mix.shape[1]
    f2 = 2 * f
    h = mxq(x, 1, "e4m3") @ unpack4(w_words, w_scales)
    hh = h[:, f:f2]
    hi = h[:, f2:]
    t = src_scale[:, None] * h[:, :f2]
    p = mxq(adj, 1, "e4m3") @ mxq(t, 0, "e4m3")
    pl = p[:, :f]
    ph = p[:, f:]
    c0 = np.maximum(pl, 0.0)
    c1 = np.maximum(hh - ph, 0.0)
    c2 = np.maximum(hi, 0.0)
    s0 = np.sum(c0 * mix[0][None, :], axis=1)
    s1 = np.sum(c1 * mix[1][None, :], axis=1)
    s2 = np.sum(c2 * mix[2][None, :], axis=1)
    score = np.stack([s0, s1, s2], axis=1)
    alpha = softmax(score)
    return alpha[:, 0:1] * c0 + alpha[:, 1:2] * c1 + alpha[:, 2:3] * c2


def setup_inputs():
    drawn = draw0()
    full = np.asarray(drawn['adj']).astype(np.float64)
    scale = (np.abs(full).reshape(1024, 8, 128).max(axis=(2,)) / 448.0).astype(np.float32)
    given = {}
    for key, value in drawn.items():
        if key == 'adj':
            given['adj_bytes'] = e4m3fn_bytes(full / np.repeat(scale.astype(np.float64), 128, axis=1))
            given['adj_scale'] = scale
        else:
            given[key] = value
    return given


def reference(x, w_words, w_scales, adj_bytes, adj_scale, src_scale, mix):
    return core(x, w_words, w_scales, e4m3fn_values(adj_bytes) * np.repeat(adj_scale.astype(np.float64), 128, axis=1), src_scale, mix)

@@ -1,0 +1,337 @@
+from contextlib import ExitStack
+
+import concourse.mybir as mybir
+from concourse.masks import make_identity
+
+N, D, F = 1024, 512, 512
+FLOPS = 2 * N * D * 3 * F + 2 * N * N * 2 * F
+
+F32 = mybir.dt.float32
+BF16 = mybir.dt.bfloat16
+U32 = mybir.dt.uint32
+I32 = mybir.dt.int32
+U8 = mybir.dt.uint8
+FP8 = mybir.dt.float8_e4m3fn
+FP8X4 = mybir.dt.float8_e4m3fn_x4
+FP4X4 = mybir.dt.float4_e2m1fn_x4
+ACT = mybir.ActivationFunctionType
+ALU = mybir.AluOpType
+AX = mybir.AxisListType
+
+P = 128
+G = 2
+T = 4
+BLK = 128
+NBLK = N // BLK
+
+
+NT = G * T
+VB = 4
+
+
+def tile_acmgnnthreefilterchannelmixing_d1p_kernel(
+    tc, x, w_words, w_scales, adj_bytes, adj_scale, src_scale, mix, out
+):
+    nc = tc.nc
+    with ExitStack() as ctx:
+        keep = ctx.enter_context(tc.tile_pool(name="keep", bufs=1))
+        work = ctx.enter_context(tc.tile_pool(name="work", bufs=3))
+        psum = ctx.enter_context(tc.psum_pool(name="psum", bufs=1))
+
+        xv = x.rearrange("(g p t) k -> g p t k", p=P, t=T)
+        av = adj_bytes.rearrange("(g p t) k -> g p t k", p=P, t=T)
+        x_sb, a_bytes = [], []
+        for g in range(G):
+            xt_ = keep.tile([P, T, D], BF16, name="x_sb%d" % g, align_bytes=64)
+            x_sb.append(xt_)
+            ab = keep.tile([P, T, N], U8, name="a_bytes%d" % g, align_bytes=64)
+            a_bytes.append(ab)
+        w_sb = keep.tile([P, 6 * F], U8, name="w_sb", align_bytes=64)
+        w_sc = keep.tile([P, 3 * F], U8, name="w_sc", align_bytes=64)
+        src_bf = keep.tile([P, G, T], BF16, name="src_bf")
+        a_scale = keep.tile([P, G, T, NBLK], F32, name="a_scale")
+        mix_sb = keep.tile([P, 3, F], BF16, name="mix_sb", align_bytes=64)
+        nc.vector.memset(w_sc[:].bitcast(I32), 0)
+        nc.sync.dma_start(out=x_sb[0][:, 0:2, :], in_=xv[0][:, 0:2, :])
+        nc.sync.dma_start(out=x_sb[0][:, 2:4, :], in_=xv[0][:, 2:4, :])
+        nc.sync.dma_start(out=w_sb[:].bitcast(I32), in_=w_words[0].bitcast(I32))
+        nc.sync.dma_start(out=a_bytes[0][:, 0:2, :], in_=av[0][:, 0:2, :])
+        nc.sync.dma_start(out=x_sb[1][:], in_=xv[1])
+        nc.sync.dma_start(out=a_bytes[0][:, 2:4, :], in_=av[0][:, 2:4, :])
+        nc.sync.dma_start(out=mix_sb[:].rearrange("p c f -> p (c f)"), in_=mix.rearrange("c f -> (c f)").partition_broadcast(P))
+        nc.sync.dma_start(out=a_bytes[1][:], in_=av[1])
+        nc.scalar.dma_start(out=a_scale[:], in_=adj_scale.rearrange("(g p t) j -> p g t j", p=P, t=T))
+        nc.scalar.dma_start(out=src_bf[:], in_=src_scale.rearrange("(g p t) -> p g t", p=P, t=T))
+        for q in range(4):
+            nc.scalar.dma_start(
+                out=w_sc[32 * q : 32 * q + 4, :].bitcast(I32),
+                in_=w_scales[0, 4 * q : 4 * q + 4, :].bitcast(I32),
+            )
+
+        ident = keep.tile([P, P], F32, name="ident")
+        make_identity(nc, ident[:])
+        warm = keep.tile([P, 1], F32, name="warm")
+        nc.vector.memset(warm[:], 0.0)
+        warm2 = keep.tile([P, 1], F32, name="warm2")
+        nc.scalar.activation(out=warm2[:], in_=warm[:], func=ACT.Exp)
+        src = keep.tile([P, 2, G * T], F32, name="src")
+        nc.vector.tensor_copy(out=src[:, 0, :], in_=src_bf[:].rearrange("p g t -> p (g t)"))
+        nc.vector.tensor_scalar(
+            out=src[:, 1, :], in0=src_bf[:].rearrange("p g t -> p (g t)"), scalar1=-1.0, scalar2=None, op0=ALU.mult
+        )
+
+        xq, xs, xi = [], [], []
+        for g in range(G):
+            xi.append(keep.tile([P, T * P * 4], BF16, name="xi%d" % g, align_bytes=64))
+            xq.append(keep.tile([P, T * P], U32, name="xq%d" % g, align_bytes=64))
+            xs.append(keep.tile([P, T * P], U8, name="xs%d" % g, align_bytes=64))
+        raw, ti, tq, ts = {}, {}, {}, {}
+        for g in range(G):
+            for c in range(2):
+                raw[g, c] = keep.tile([P, T, F], BF16, name="raw%d%d" % (g, c), align_bytes=64)
+                ti[g, c] = keep.tile([P, F, T], BF16, name="ti%d%d" % (g, c), align_bytes=64)
+                tq[g, c] = keep.tile([P, F], U32, name="tq%d%d" % (g, c), align_bytes=64)
+                ts[g, c] = keep.tile([P, F], U8, name="ts%d%d" % (g, c), align_bytes=64)
+        aw, ai, aq, as_, score = [], [], [], [], []
+        for i in range(G * T):
+            aw.append(keep.tile([P, N], BF16, name="aw%d" % i, align_bytes=64))
+            ai.append(keep.tile([P, 2 * P * 4], BF16, name="ai%d" % i, align_bytes=64))
+            aq.append(keep.tile([P, 2 * P], U32, name="aq%d" % i, align_bytes=64))
+            as_.append(keep.tile([P, 2 * P], U8, name="as%d" % i, align_bytes=64))
+            score.append(keep.tile([P, 3], F32, name="score%d" % i))
+
+        def bank_of(tag, bufs):
+            b = psum.tile([P, 512], F32, name="b_" + tag, tag=tag, bufs=bufs)
+            return b
+
+        def main():
+            return bank_of("main", 5)
+
+        def turn_x(g, h, copy):
+            bank = main()
+            bv = bank[:].rearrange("p (j u r) -> p j u r", j=2, u=2)
+            for j in range(2):
+                words = x_sb[g][:, 2 * h + j, :].bitcast(F32)
+                for u in range(2):
+                    nc.tensor.transpose(bv[:, j, u, :], words[:, u : D // 2 : 2], ident[:])
+            xiw = xi[g][:].bitcast(F32).rearrange("p (t r u) -> p t r u", t=T, u=2)
+            copy(out=xiw[:, 2 * h : 2 * h + 2], in_=bv.rearrange("p j u r -> p j r u"))
+
+        def quant_x(g, h):
+            cols = slice(2 * h * P, 2 * (h + 1) * P)
+            nc.vector.quantize_mx(
+                out=xq[g][:, cols].bitcast(FP8X4), scales=xs[g][:, cols], in_=xi[g][:, 8 * h * P : 8 * (h + 1) * P]
+            )
+
+        def project(bank, i, c, start, stop):
+            g, t = divmod(i, T)
+            nc.tensor.matmul_mx(
+                out=bank,
+                lhsT=xq[g][:, t * P : (t + 1) * P].bitcast(FP8X4),
+                lhsT_scale=xs[g][:, t * P : (t + 1) * P],
+                rhs=w_sb[:, 2 * F * c : 2 * F * (c + 1)].bitcast(FP4X4),
+                rhs_scale=w_sc[:, F * c : F * (c + 1)],
+                start=start,
+                stop=stop,
+            )
+
+        def source(g, c, t, on_vector):
+            hb = main()
+            project(hb[:], g * T + t, c, True, True)
+            s = src[:, c, g * T + t : g * T + t + 1]
+            if on_vector:
+                nc.vector.tensor_scalar(out=raw[g, c][:, t, :], in0=hb[:], scalar1=s, scalar2=None, op0=ALU.mult)
+            else:
+                nc.scalar.activation(out=raw[g, c][:, t, :], in_=hb[:], func=ACT.Copy, scale=s)
+
+        def interleave(g, c):
+            nc.vector.tensor_copy(out=ti[g, c][:], in_=raw[g, c][:].rearrange("p t f -> p f t"))
+
+        def quant_t(g, c):
+            nc.vector.quantize_mx(
+                out=tq[g, c][:].bitcast(FP8X4), scales=ts[g, c][:], in_=ti[g, c][:].rearrange("p f t -> p (f t)")
+            )
+
+        def widen(i, on_vector, j0=0, j1=NBLK):
+            g, t = divmod(i, T)
+            for j in range(j0, j1):
+                cols = slice(j * BLK, (j + 1) * BLK)
+                s = a_scale[:, g, t, j : j + 1]
+                src8 = a_bytes[g][:, t, cols].bitcast(FP8)
+                if on_vector:
+                    nc.vector.tensor_scalar(out=aw[i][:, cols], in0=src8, scalar1=s, scalar2=None, op0=ALU.mult)
+                else:
+                    nc.scalar.activation(out=aw[i][:, cols], in_=src8, func=ACT.Copy, scale=s)
+
+        turned = {}
+
+        def turn_a(i):
+            words = aw[i][:].bitcast(F32)
+            bank = bank_of("turn", 1)
+            bv = bank[:].rearrange("p (q u r) -> p q u r", q=2, u=2)
+            for q in range(2):
+                for u in range(2):
+                    nc.tensor.transpose(bv[:, q, u, :], words[:, 256 * q + u : 256 * (q + 1) : 2], ident[:])
+            turned[i] = bv
+
+        def take_a(i, copy):
+            copy(
+                out=ai[i][:].bitcast(F32).rearrange("p (q r u) -> p q r u", q=2, u=2),
+                in_=turned[i].rearrange("p q u r -> p q r u"),
+            )
+
+        def quant_a(i):
+            nc.vector.quantize_mx(out=aq[i][:].bitcast(FP8X4), scales=as_[i][:], in_=ai[i][:])
+
+        banks = {}
+
+        def rate(i, c):
+            junk = work.tile([P, F], F32, name="junk")
+            nc.vector.scalar_tensor_tensor(
+                out=junk[:], in0=banks[i, c][:], scalar=0.0, in1=mix_sb[:, c, :], op0=ALU.max, op1=ALU.mult,
+                accum_out=score[i][:, c : c + 1],
+            )
+
+        def identity_channel(i):
+            banks[i, 2] = bank_of("id", 2)
+            project(banks[i, 2][:], i, 2, True, True)
+
+        def propagate(i):
+            for c in range(2):
+                banks[i, c] = main()
+                pb = banks[i, c]
+                if c == 1:
+                    project(pb[:], i, 1, True, False)
+                for q in range(2):
+                    nc.tensor.matmul_mx(
+                        out=pb[:],
+                        lhsT=aq[i][:, q * P : (q + 1) * P].bitcast(FP8X4),
+                        lhsT_scale=as_[i][:, q * P : (q + 1) * P],
+                        rhs=tq[q, c][:].bitcast(FP8X4),
+                        rhs_scale=ts[q, c][:],
+                        start=(c == 0 and q == 0),
+                        stop=(q == 1),
+                    )
+
+        dif, ex, tot, al = {}, {}, {}, {}
+
+        tops = {}
+
+        def top(i):
+            tops[i] = work.tile([P, 1], F32, name="top")
+            nc.vector.reduce_max(out=tops[i][:], in_=score[i][:], axis=AX.X)
+
+        def soft_a(i):
+            dif[i] = work.tile([P, 3], F32, name="dif")
+            nc.vector.tensor_scalar(out=dif[i][:], in0=score[i][:], scalar1=tops[i][:], scalar2=None, op0=ALU.subtract)
+
+        def soft_b(i):
+            ex[i] = work.tile([P, 3], F32, name="ex")
+            tot[i] = work.tile([P, 1], F32, name="tot")
+            nc.scalar.activation(out=ex[i][:], in_=dif[i][:], func=ACT.Exp, accum_out=tot[i][:])
+
+        def soft_c(i):
+            inv = work.tile([P, 1], F32, name="inv")
+            nc.vector.reciprocal(out=inv[:], in_=tot[i][:])
+            al[i] = work.tile([P, 3], F32, name="al")
+            nc.vector.tensor_scalar(out=al[i][:], in0=ex[i][:], scalar1=inv[:], scalar2=None, op0=ALU.mult)
+
+        ov = out.rearrange("(g p t) f -> g t p f", p=P, t=T)
+        r = {}
+
+        def weigh(i, c, on_vector=False):
+            r[i, c] = work.tile([P, F], F32, name="r%d" % c)
+            if on_vector:
+                nc.vector.tensor_scalar(
+                    out=r[i, c][:], in0=banks[i, c][:], scalar1=0.0, scalar2=al[i][:, c : c + 1], op0=ALU.max, op1=ALU.mult
+                )
+            else:
+                nc.scalar.activation(out=r[i, c][:], in_=banks[i, c][:], func=ACT.Relu, scale=al[i][:, c : c + 1])
+
+        part = {}
+
+        def add_a(i, eng):
+            part[i] = work.tile([P, F], F32, name="o1")
+            eng.tensor_tensor(out=part[i][:], in0=r[i, 0][:], in1=r[i, 1][:], op=ALU.add)
+
+        def add_b(i, eng):
+            g, t = divmod(i, T)
+            o2 = work.tile([P, F], F32, name="o2")
+            eng.tensor_tensor(out=o2[:], in0=part[i][:], in1=r[i, 2][:], op=ALU.add)
+            nc.sync.dma_start(out=ov[g, t], in_=o2[:])
+
+        sc, ve, gp, ve2 = nc.scalar.copy, nc.vector.tensor_copy, nc.gpsimd, nc.vector
+        with tc.manual_schedule():
+            turn_x(0, 0, sc)
+            quant_x(0, 0)
+            turn_x(0, 1, ve)
+            quant_x(0, 1)
+            for t in range(T):
+                source(0, 0, t, False)
+            widen(0, True)
+            turn_x(1, 0, sc)
+            turn_x(1, 1, ve)
+            quant_x(1, 0)
+            quant_x(1, 1)
+            for t in range(T):
+                source(0, 1, t, False)
+            widen(1, True)
+            interleave(0, 0)
+            turn_a(0)
+            for t in range(T):
+                source(1, 0, t, False)
+            quant_t(0, 0)
+            interleave(0, 1)
+            take_a(0, sc)
+            turn_a(1)
+            for t in range(T):
+                source(1, 1, t, False)
+            quant_a(0)
+            quant_t(0, 1)
+            take_a(1, sc)
+            identity_channel(0)
+            interleave(1, 0)
+            rate(0, 2)
+            quant_t(1, 0)
+            quant_a(1)
+            widen(2, False)
+            interleave(1, 1)
+            quant_t(1, 1)
+            propagate(0)
+            widen(3, False, 0, 4)
+            turn_a(2)
+            take_a(2, sc)
+            widen(3, False, 4, 8)
+            for s in range(NT + 1):
+                last = s == NT
+                if s > 0:
+                    identity_channel(s - 1)
+                    weigh(s - 1, 0)
+                    weigh(s - 1, 1, last)
+                    weigh(s - 1, 2)
+                    add_a(s - 1, ve2 if last else gp)
+                    add_b(s - 1, ve2 if last else gp)
+                if s + 1 < NT:
+                    identity_channel(s + 1)
+                if s < NT:
+                    rate(s, 0)
+                    rate(s, 1)
+                if s + 1 < NT:
+                    rate(s + 1, 2)
+                if s < NT:
+                    top(s)
+                if s + 2 < NT:
+                    quant_a(s + 2)
+                if s < NT:
+                    soft_a(s)
+                    soft_b(s)
+                if s + 3 < NT:
+                    turn_a(s + 3)
+                    take_a(s + 3, sc)
+                if s + 4 < NT:
+                    widen(s + 4, True, 0, VB)
+                    widen(s + 4, False, VB, NBLK)
+                if s < NT:
+                    soft_c(s)
+                if s + 1 < NT:
+                    propagate(s + 1)

@@ -26,7 +26,8 @@ NBLK = N // BLK
 
 
 NT = G * T
-VB = 4
+VB = 0
+SPREAD = 46.0
 
 
 def tile_acmgnnthreefilterchannelmixing_d1p_kernel(
@@ -52,13 +53,14 @@ def tile_acmgnnthreefilterchannelmixing_d1p_kernel(
         a_scale = keep.tile([P, G, T, NBLK], F32, name="a_scale")
         mix_sb = keep.tile([P, 3, F], BF16, name="mix_sb", align_bytes=64)
         nc.vector.memset(w_sc[:].bitcast(I32), 0)
+        nc.sync.dma_start(out=a_bytes[0][:, 0:1, :], in_=av[0][:, 0:1, :])
         nc.sync.dma_start(out=x_sb[0][:, 0:2, :], in_=xv[0][:, 0:2, :])
         nc.sync.dma_start(out=x_sb[0][:, 2:4, :], in_=xv[0][:, 2:4, :])
         nc.sync.dma_start(out=w_sb[:].bitcast(I32), in_=w_words[0].bitcast(I32))
-        nc.sync.dma_start(out=a_bytes[0][:, 0:2, :], in_=av[0][:, 0:2, :])
+        nc.sync.dma_start(out=a_bytes[0][:, 1:2, :], in_=av[0][:, 1:2, :])
         nc.sync.dma_start(out=x_sb[1][:], in_=xv[1])
-        nc.sync.dma_start(out=a_bytes[0][:, 2:4, :], in_=av[0][:, 2:4, :])
         nc.sync.dma_start(out=mix_sb[:].rearrange("p c f -> p (c f)"), in_=mix.rearrange("c f -> (c f)").partition_broadcast(P))
+        nc.sync.dma_start(out=a_bytes[0][:, 2:4, :], in_=av[0][:, 2:4, :])
         nc.sync.dma_start(out=a_bytes[1][:], in_=av[1])
         nc.scalar.dma_start(out=a_scale[:], in_=adj_scale.rearrange("(g p t) j -> p g t j", p=P, t=T))
         nc.scalar.dma_start(out=src_bf[:], in_=src_scale.rearrange("(g p t) -> p g t", p=P, t=T))
@@ -80,6 +82,11 @@ def tile_acmgnnthreefilterchannelmixing_d1p_kernel(
             out=src[:, 1, :], in0=src_bf[:].rearrange("p g t -> p (g t)"), scalar1=-1.0, scalar2=None, op0=ALU.mult
         )
 
+        mix_neg = keep.tile([P, 3, F], BF16, name="mix_neg", align_bytes=64)
+        nc.gpsimd.tensor_scalar(
+            out=mix_neg[:], in0=mix_sb[:], scalar1=-1.0, scalar2=0.0, op0=ALU.mult, op1=ALU.add
+        )
+
         xq, xs, xi = [], [], []
         for g in range(G):
             xi.append(keep.tile([P, T * P * 4], BF16, name="xi%d" % g, align_bytes=64))
@@ -98,7 +105,7 @@ def tile_acmgnnthreefilterchannelmixing_d1p_kernel(
             ai.append(keep.tile([P, 2 * P * 4], BF16, name="ai%d" % i, align_bytes=64))
             aq.append(keep.tile([P, 2 * P], U32, name="aq%d" % i, align_bytes=64))
             as_.append(keep.tile([P, 2 * P], U8, name="as%d" % i, align_bytes=64))
-            score.append(keep.tile([P, 3], F32, name="score%d" % i))
+            score.append(keep.tile([P, 5], F32, name="score%d" % i))
 
         def bank_of(tag, bufs):
             b = psum.tile([P, 512], F32, name="b_" + tag, tag=tag, bufs=bufs)
@@ -188,7 +195,7 @@ def tile_acmgnnthreefilterchannelmixing_d1p_kernel(
         def rate(i, c):
             junk = work.tile([P, F], F32, name="junk")
             nc.vector.scalar_tensor_tensor(
-                out=junk[:], in0=banks[i, c][:], scalar=0.0, in1=mix_sb[:, c, :], op0=ALU.max, op1=ALU.mult,
+                out=junk[:], in0=banks[i, c][:], scalar=0.0, in1=mix_neg[:, c, :], op0=ALU.max, op1=ALU.mult,
                 accum_out=score[i][:, c : c + 1],
             )
 
@@ -213,125 +220,147 @@ def tile_acmgnnthreefilterchannelmixing_d1p_kernel(
                         stop=(q == 1),
                     )
 
-        dif, ex, tot, al = {}, {}, {}, {}
+        low, w, tot, inv, a1 = {}, {}, {}, {}, {}
 
-        tops = {}
+        def soft_o(i):
+            nc.vector.tensor_scalar(
+                out=score[i][:, 3:5], in0=score[i][:, 0:2], scalar1=SPREAD, scalar2=None, op0=ALU.add
+            )
 
-        def top(i):
-            tops[i] = work.tile([P, 1], F32, name="top")
-            nc.vector.reduce_max(out=tops[i][:], in_=score[i][:], axis=AX.X)
+        def soft_m(i):
+            low[i] = work.tile([P, 1], F32, name="low")
+            nc.vector.tensor_reduce(out=low[i][:], in_=score[i][:, 2:5], axis=AX.X, op=ALU.min)
+
+        def soft_e(i):
+            w[i] = work.tile([P, 3], F32, name="w")
+            tot[i] = work.tile([P, 1], F32, name="tot")
+            nc.scalar.activation(
+                out=w[i][:], in_=score[i][:, 0:3], func=ACT.Exp, bias=low[i][:], scale=-1.0, accum_out=tot[i][:]
+            )
+
+        def soft_i(i):
+            inv[i] = work.tile([P, 1], F32, name="inv")
+            nc.vector.reciprocal(out=inv[i][:], in_=tot[i][:])
 
         def soft_a(i):
-            dif[i] = work.tile([P, 3], F32, name="dif")
-            nc.vector.tensor_scalar(out=dif[i][:], in0=score[i][:], scalar1=tops[i][:], scalar2=None, op0=ALU.subtract)
-
-        def soft_b(i):
-            ex[i] = work.tile([P, 3], F32, name="ex")
-            tot[i] = work.tile([P, 1], F32, name="tot")
-            nc.scalar.activation(out=ex[i][:], in_=dif[i][:], func=ACT.Exp, accum_out=tot[i][:])
-
-        def soft_c(i):
-            inv = work.tile([P, 1], F32, name="inv")
-            nc.vector.reciprocal(out=inv[:], in_=tot[i][:])
-            al[i] = work.tile([P, 3], F32, name="al")
-            nc.vector.tensor_scalar(out=al[i][:], in0=ex[i][:], scalar1=inv[:], scalar2=None, op0=ALU.mult)
+            a1[i] = work.tile([P, 1], F32, name="a1")
+            nc.scalar.activation(out=a1[i][:], in_=w[i][:, 1:2], func=ACT.Copy, scale=inv[i][:])
 
         ov = out.rearrange("(g p t) f -> g t p f", p=P, t=T)
-        r = {}
+        r, y = {}, {}
 
-        def weigh(i, c, on_vector=False):
-            r[i, c] = work.tile([P, F], F32, name="r%d" % c)
-            if on_vector:
-                nc.vector.tensor_scalar(
-                    out=r[i, c][:], in0=banks[i, c][:], scalar1=0.0, scalar2=al[i][:, c : c + 1], op0=ALU.max, op1=ALU.mult
-                )
-            else:
-                nc.scalar.activation(out=r[i, c][:], in_=banks[i, c][:], func=ACT.Relu, scale=al[i][:, c : c + 1])
+        def weigh(i, c, cols=slice(0, F)):
+            if cols.start == 0:
+                r[i, c] = work.tile([P, F], F32, name="r%d" % c)
+            s = w[i][:, 0:1] if c == 0 else a1[i][:]
+            nc.scalar.activation(out=r[i, c][:, cols], in_=banks[i, c][:, cols], func=ACT.Relu, scale=s)
 
-        part = {}
+        o = {}
 
-        def add_a(i, eng):
-            part[i] = work.tile([P, F], F32, name="o1")
-            eng.tensor_tensor(out=part[i][:], in0=r[i, 0][:], in1=r[i, 1][:], op=ALU.add)
+        def add_a(i, cols=slice(0, F)):
+            if cols.start == 0:
+                y[i] = work.tile([P, F], F32, name="y")
+            nc.vector.scalar_tensor_tensor(
+                out=y[i][:, cols], in0=banks[i, 2][:, cols], scalar=0.0, in1=r[i, 0][:, cols], op0=ALU.max, op1=ALU.add
+            )
 
-        def add_b(i, eng):
+        def add_b(i, cols=slice(0, F)):
             g, t = divmod(i, T)
-            o2 = work.tile([P, F], F32, name="o2")
-            eng.tensor_tensor(out=o2[:], in0=part[i][:], in1=r[i, 2][:], op=ALU.add)
-            nc.sync.dma_start(out=ov[g, t], in_=o2[:])
+            if cols.start == 0:
+                o[i] = work.tile([P, F], F32, name="o")
+            nc.vector.scalar_tensor_tensor(
+                out=o[i][:, cols], in0=y[i][:, cols], scalar=inv[i][:], in1=r[i, 1][:, cols], op0=ALU.mult, op1=ALU.add
+            )
+            nc.sync.dma_start(out=ov[g, t][:, cols], in_=o[i][:, cols])
 
-        sc, ve, gp, ve2 = nc.scalar.copy, nc.vector.tensor_copy, nc.gpsimd, nc.vector
+        sc, ve = nc.scalar.copy, nc.vector.tensor_copy
         with tc.manual_schedule():
+            widen(0, True)
             turn_x(0, 0, sc)
             quant_x(0, 0)
-            turn_x(0, 1, ve)
+            turn_x(0, 1, sc)
             quant_x(0, 1)
+            widen(1, True, 0, 6)
             for t in range(T):
                 source(0, 0, t, False)
-            widen(0, True)
-            turn_x(1, 0, sc)
-            turn_x(1, 1, ve)
+            turn_x(1, 0, ve)
+            turn_x(1, 1, sc)
             quant_x(1, 0)
             quant_x(1, 1)
             for t in range(T):
                 source(0, 1, t, False)
-            widen(1, True)
             interleave(0, 0)
-            turn_a(0)
+            identity_channel(0)
+            rate(0, 2)
+            quant_t(0, 0)
             for t in range(T):
                 source(1, 0, t, False)
-            quant_t(0, 0)
+            identity_channel(1)
+            rate(1, 2)
             interleave(0, 1)
+            turn_a(0)
             take_a(0, sc)
-            turn_a(1)
+            identity_channel(2)
+            rate(2, 2)
+            quant_t(0, 1)
+            widen(1, False, 6, 8)
             for t in range(T):
                 source(1, 1, t, False)
-            quant_a(0)
-            quant_t(0, 1)
-            take_a(1, sc)
-            identity_channel(0)
             interleave(1, 0)
-            rate(0, 2)
+            quant_a(0)
+            turn_a(1)
+            take_a(1, sc)
             quant_t(1, 0)
-            quant_a(1)
+            identity_channel(3)
+            rate(3, 2)
             widen(2, False)
             interleave(1, 1)
+            quant_a(1)
+            turn_a(2)
             quant_t(1, 1)
             propagate(0)
-            widen(3, False, 0, 4)
-            turn_a(2)
             take_a(2, sc)
-            widen(3, False, 4, 8)
-            for s in range(NT + 1):
-                last = s == NT
+            widen(3, False)
+            for s in range(NT):
+                if 1 < s and s + 2 < NT:
+                    widen(s + 2, False)
+                if s > 0:
+                    weigh(s - 1, 0)
+                    soft_a(s - 1)
+                    weigh(s - 1, 1)
+                rate(s, 0)
+                rate(s, 1)
+                if s == NT - 1:
+                    soft_o(s)
+                    soft_m(s)
                 if s > 0:
                     identity_channel(s - 1)
-                    weigh(s - 1, 0)
-                    weigh(s - 1, 1, last)
-                    weigh(s - 1, 2)
-                    add_a(s - 1, ve2 if last else gp)
-                    add_b(s - 1, ve2 if last else gp)
-                if s + 1 < NT:
-                    identity_channel(s + 1)
-                if s < NT:
-                    rate(s, 0)
-                    rate(s, 1)
-                if s + 1 < NT:
-                    rate(s + 1, 2)
-                if s < NT:
-                    top(s)
+                    add_a(s - 1)
+                if s < NT - 1:
+                    soft_o(s)
+                if s > 0:
+                    add_b(s - 1)
+                if s < NT - 1:
+                    soft_m(s)
+                if 4 <= s + 3 < NT:
+                    identity_channel(s + 3)
+                    rate(s + 3, 2)
+                if 0 < s and s + 2 < NT:
+                    turn_a(s + 2)
+                    take_a(s + 2, sc)
+                soft_e(s)
                 if s + 2 < NT:
                     quant_a(s + 2)
-                if s < NT:
-                    soft_a(s)
-                    soft_b(s)
-                if s + 3 < NT:
-                    turn_a(s + 3)
-                    take_a(s + 3, sc)
-                if s + 4 < NT:
-                    widen(s + 4, True, 0, VB)
-                    widen(s + 4, False, VB, NBLK)
-                if s < NT:
-                    soft_c(s)
+                soft_i(s)
                 if s + 1 < NT:
                     propagate(s + 1)
+            i = NT - 1
+            identity_channel(i)
+            halves = (slice(0, F // 2), slice(F // 2, F))
+            for cols in halves:
+                weigh(i, 0, cols)
+                add_a(i, cols)
+            soft_a(i)
+            for cols in halves:
+                weigh(i, 1, cols)
+                add_b(i, cols)

@@ -26,7 +26,11 @@ NBLK = N // BLK
 
 
 NT = G * T
-VB = 0
+VB = 1
+R3 = 4
+RAWV = 4
+REST = 8
+AHEAD = 99
 SPREAD = 46.0
 
 
@@ -51,6 +55,10 @@ def tile_acmgnnthreefilterchannelmixing_d1p_kernel(
         w_sc = keep.tile([P, 3 * F], U8, name="w_sc", align_bytes=64)
         src_bf = keep.tile([P, G, T], BF16, name="src_bf")
         a_scale = keep.tile([P, G, T, NBLK], F32, name="a_scale")
+        mix_row = keep.tile([P, F], BF16, name="mix_row", align_bytes=64)
+        nc.vector.memset(mix_row[:].bitcast(I32), 0)
+        ones = keep.tile([P, P], BF16, name="ones", align_bytes=64)
+        nc.gpsimd.memset(ones[:], 1.0)
         mix_sb = keep.tile([P, 3, F], BF16, name="mix_sb", align_bytes=64)
         nc.vector.memset(w_sc[:].bitcast(I32), 0)
         nc.sync.dma_start(out=a_bytes[0][:, 0:1, :], in_=av[0][:, 0:1, :])
@@ -59,9 +67,13 @@ def tile_acmgnnthreefilterchannelmixing_d1p_kernel(
         nc.sync.dma_start(out=w_sb[:].bitcast(I32), in_=w_words[0].bitcast(I32))
         nc.sync.dma_start(out=a_bytes[0][:, 1:2, :], in_=av[0][:, 1:2, :])
         nc.sync.dma_start(out=x_sb[1][:], in_=xv[1])
-        nc.sync.dma_start(out=mix_sb[:].rearrange("p c f -> p (c f)"), in_=mix.rearrange("c f -> (c f)").partition_broadcast(P))
         nc.sync.dma_start(out=a_bytes[0][:, 2:4, :], in_=av[0][:, 2:4, :])
         nc.sync.dma_start(out=a_bytes[1][:], in_=av[1])
+        nc.sync.dma_start(
+            out=mix_sb[:, 0:2, :].rearrange("p c f -> p (c f)"),
+            in_=mix[0:2, :].rearrange("c f -> (c f)").partition_broadcast(P),
+        )
+        nc.scalar.dma_start(out=mix_row[0:1, :], in_=mix[2:3, :])
         nc.scalar.dma_start(out=a_scale[:], in_=adj_scale.rearrange("(g p t) j -> p g t j", p=P, t=T))
         nc.scalar.dma_start(out=src_bf[:], in_=src_scale.rearrange("(g p t) -> p g t", p=P, t=T))
         for q in range(4):
@@ -80,11 +92,6 @@ def tile_acmgnnthreefilterchannelmixing_d1p_kernel(
         nc.vector.tensor_copy(out=src[:, 0, :], in_=src_bf[:].rearrange("p g t -> p (g t)"))
         nc.vector.tensor_scalar(
             out=src[:, 1, :], in0=src_bf[:].rearrange("p g t -> p (g t)"), scalar1=-1.0, scalar2=None, op0=ALU.mult
-        )
-
-        mix_neg = keep.tile([P, 3, F], BF16, name="mix_neg", align_bytes=64)
-        nc.gpsimd.tensor_scalar(
-            out=mix_neg[:], in0=mix_sb[:], scalar1=-1.0, scalar2=0.0, op0=ALU.mult, op1=ALU.add
         )
 
         xq, xs, xi = [], [], []
@@ -113,6 +120,11 @@ def tile_acmgnnthreefilterchannelmixing_d1p_kernel(
 
         def main():
             return bank_of("main", 5)
+
+        def spread_mix(c, copy):
+            bank = main()
+            nc.tensor.matmul(bank[:], lhsT=ones[:], rhs=mix_row[:], start=True, stop=True)
+            copy(out=mix_sb[:, c, :], in_=bank[:])
 
         def turn_x(g, h, copy):
             bank = main()
@@ -152,7 +164,16 @@ def tile_acmgnnthreefilterchannelmixing_d1p_kernel(
                 nc.scalar.activation(out=raw[g, c][:, t, :], in_=hb[:], func=ACT.Copy, scale=s)
 
         def interleave(g, c):
-            nc.vector.tensor_copy(out=ti[g, c][:], in_=raw[g, c][:].rearrange("p t f -> p f t"))
+            nc.vector.tensor_copy(
+                out=ti[g, c][:].rearrange("p (c i) t -> p c t i", i=4),
+                in_=raw[g, c][:].rearrange("p t (c i) -> p c t i", i=4),
+            )
+
+        def interleave_gp(g, c):
+            nc.gpsimd.tensor_scalar(
+                out=ti[g, c][:], in0=raw[g, c][:].rearrange("p t f -> p f t"),
+                scalar1=1.0, scalar2=0.0, op0=ALU.mult, op1=ALU.add,
+            )
 
         def quant_t(g, c):
             nc.vector.quantize_mx(
@@ -195,7 +216,7 @@ def tile_acmgnnthreefilterchannelmixing_d1p_kernel(
         def rate(i, c):
             junk = work.tile([P, F], F32, name="junk")
             nc.vector.scalar_tensor_tensor(
-                out=junk[:], in0=banks[i, c][:], scalar=0.0, in1=mix_neg[:, c, :], op0=ALU.max, op1=ALU.mult,
+                out=junk[:], in0=banks[i, c][:], scalar=0.0, in1=mix_sb[:, c, :], op0=ALU.max, op1=ALU.mult,
                 accum_out=score[i][:, c : c + 1],
             )
 
@@ -224,18 +245,18 @@ def tile_acmgnnthreefilterchannelmixing_d1p_kernel(
 
         def soft_o(i):
             nc.vector.tensor_scalar(
-                out=score[i][:, 3:5], in0=score[i][:, 0:2], scalar1=SPREAD, scalar2=None, op0=ALU.add
+                out=score[i][:, 3:5], in0=score[i][:, 0:2], scalar1=SPREAD, scalar2=None, op0=ALU.subtract
             )
 
         def soft_m(i):
             low[i] = work.tile([P, 1], F32, name="low")
-            nc.vector.tensor_reduce(out=low[i][:], in_=score[i][:, 2:5], axis=AX.X, op=ALU.min)
+            nc.vector.tensor_reduce(out=low[i][:], in_=score[i][:, 2:5], axis=AX.X, op=ALU.max, negate=True)
 
         def soft_e(i):
             w[i] = work.tile([P, 3], F32, name="w")
             tot[i] = work.tile([P, 1], F32, name="tot")
             nc.scalar.activation(
-                out=w[i][:], in_=score[i][:, 0:3], func=ACT.Exp, bias=low[i][:], scale=-1.0, accum_out=tot[i][:]
+                out=w[i][:], in_=score[i][:, 0:3], func=ACT.Exp, bias=low[i][:], accum_out=tot[i][:]
             )
 
         def soft_i(i):
@@ -275,59 +296,66 @@ def tile_acmgnnthreefilterchannelmixing_d1p_kernel(
 
         sc, ve = nc.scalar.copy, nc.vector.tensor_copy
         with tc.manual_schedule():
-            widen(0, True)
+            spread_mix(2, sc)
             turn_x(0, 0, sc)
+            widen(0, True)
             quant_x(0, 0)
             turn_x(0, 1, sc)
             quant_x(0, 1)
-            widen(1, True, 0, 6)
-            for t in range(T):
+            for t in range(2):
                 source(0, 0, t, False)
-            turn_x(1, 0, ve)
+                identity_channel(t)
+                rate(t, 2)
+            turn_x(1, 0, sc)
             turn_x(1, 1, sc)
             quant_x(1, 0)
             quant_x(1, 1)
+            for t in range(2, T):
+                source(0, 0, t, False)
             for t in range(T):
                 source(0, 1, t, False)
+                if t < R3:
+                    identity_channel(2 + t)
+                    rate(2 + t, 2)
             interleave(0, 0)
-            identity_channel(0)
-            rate(0, 2)
+            source(1, 0, 0, False)
+            identity_channel(2 + R3)
+            rate(2 + R3, 2)
             quant_t(0, 0)
-            for t in range(T):
-                source(1, 0, t, False)
-            identity_channel(1)
-            rate(1, 2)
             interleave(0, 1)
+            source(1, 0, 1, False)
+            identity_channel(3 + R3)
+            rate(3 + R3, 2)
+            for t in range(2, T):
+                source(1, 0, t, False)
+            quant_t(0, 1)
             turn_a(0)
             take_a(0, sc)
-            identity_channel(2)
-            rate(2, 2)
-            quant_t(0, 1)
-            widen(1, False, 6, 8)
-            for t in range(T):
-                source(1, 1, t, False)
             interleave(1, 0)
+            for t in range(T):
+                source(1, 1, t, t >= RAWV)
             quant_a(0)
+            quant_t(1, 0)
+            for i in range(4 + R3, REST):
+                identity_channel(i)
+                rate(i, 2)
+            widen(1, False)
+            interleave(1, 1)
             turn_a(1)
             take_a(1, sc)
-            quant_t(1, 0)
-            identity_channel(3)
-            rate(3, 2)
-            widen(2, False)
-            interleave(1, 1)
             quant_a(1)
-            turn_a(2)
             quant_t(1, 1)
             propagate(0)
-            take_a(2, sc)
-            widen(3, False)
+            widen(2, False)
+            turn_a(2)
+
             for s in range(NT):
-                if 1 < s and s + 2 < NT:
-                    widen(s + 2, False)
                 if s > 0:
                     weigh(s - 1, 0)
                     soft_a(s - 1)
                     weigh(s - 1, 1)
+                if s + 2 < NT:
+                    take_a(s + 2, sc)
                 rate(s, 0)
                 rate(s, 1)
                 if s == NT - 1:
@@ -342,18 +370,20 @@ def tile_acmgnnthreefilterchannelmixing_d1p_kernel(
                     add_b(s - 1)
                 if s < NT - 1:
                     soft_m(s)
-                if 4 <= s + 3 < NT:
-                    identity_channel(s + 3)
-                    rate(s + 3, 2)
-                if 0 < s and s + 2 < NT:
-                    turn_a(s + 2)
-                    take_a(s + 2, sc)
-                soft_e(s)
-                if s + 2 < NT:
-                    quant_a(s + 2)
-                soft_i(s)
                 if s + 1 < NT:
                     propagate(s + 1)
+                if s + AHEAD < NT:
+                    identity_channel(s + AHEAD)
+                    rate(s + AHEAD, 2)
+                if s + 3 < NT:
+                    widen(s + 3, True, 0, VB)
+                    widen(s + 3, False, VB, NBLK)
+                if s + 2 < NT:
+                    quant_a(s + 2)
+                soft_e(s)
+                if s + 3 < NT:
+                    turn_a(s + 3)
+                soft_i(s)
             i = NT - 1
             identity_channel(i)
             halves = (slice(0, F // 2), slice(F // 2, F))

@@ -19,19 +19,16 @@ ALU = mybir.AluOpType
 AX = mybir.AxisListType
 
 P = 128
-G = 2
-T = 4
-BLK = 128
-NBLK = N // BLK
+PACK = 4
+GROUPS = N // (P * PACK)
+TILES = GROUPS * PACK
+BANK = 512
+BLOCK = 128
+BLOCKS = N // BLOCK
+LOW, HIGH, IDENTITY = 0, 1, 2
 
-
-NT = G * T
-VB = 1
-R3 = 4
-RAWV = 4
-REST = 8
-AHEAD = 99
 SPREAD = 46.0
+VECTOR_BLOCKS = 3
 
 
 def tile_acmgnnthreefilterchannelmixing_d1p_kernel(
@@ -43,354 +40,427 @@ def tile_acmgnnthreefilterchannelmixing_d1p_kernel(
         work = ctx.enter_context(tc.tile_pool(name="work", bufs=3))
         psum = ctx.enter_context(tc.psum_pool(name="psum", bufs=1))
 
-        xv = x.rearrange("(g p t) k -> g p t k", p=P, t=T)
-        av = adj_bytes.rearrange("(g p t) k -> g p t k", p=P, t=T)
-        x_sb, a_bytes = [], []
-        for g in range(G):
-            xt_ = keep.tile([P, T, D], BF16, name="x_sb%d" % g, align_bytes=64)
-            x_sb.append(xt_)
-            ab = keep.tile([P, T, N], U8, name="a_bytes%d" % g, align_bytes=64)
-            a_bytes.append(ab)
-        w_sb = keep.tile([P, 6 * F], U8, name="w_sb", align_bytes=64)
-        w_sc = keep.tile([P, 3 * F], U8, name="w_sc", align_bytes=64)
-        src_bf = keep.tile([P, G, T], BF16, name="src_bf")
-        a_scale = keep.tile([P, G, T, NBLK], F32, name="a_scale")
+        x_rows = [keep.tile([P, PACK, D], BF16, name="x_rows%d" % g, align_bytes=64) for g in range(GROUPS)]
+        adj_codes = [keep.tile([P, PACK, N], U8, name="adj_codes%d" % g, align_bytes=64) for g in range(GROUPS)]
+        adj_factors = keep.tile([P, GROUPS, PACK, BLOCKS], F32, name="adj_factors")
+        w_codes = keep.tile([P, 2 * 3 * F], U8, name="w_codes", align_bytes=64)
+        w_scale_rows = keep.tile([P, 3 * F], U8, name="w_scale_rows", align_bytes=64)
+        factors_bf16 = keep.tile([P, TILES], BF16, name="factors_bf16")
         mix_row = keep.tile([P, F], BF16, name="mix_row", align_bytes=64)
-        nc.vector.memset(mix_row[:].bitcast(I32), 0)
+        mix_all = keep.tile([P, 3, F], BF16, name="mix_all", align_bytes=64)
+
+        eye = keep.tile([P, P], F32, name="eye")
+        make_identity(nc, eye[:])
         ones = keep.tile([P, P], BF16, name="ones", align_bytes=64)
         nc.gpsimd.memset(ones[:], 1.0)
-        mix_sb = keep.tile([P, 3, F], BF16, name="mix_sb", align_bytes=64)
-        nc.vector.memset(w_sc[:].bitcast(I32), 0)
-        nc.sync.dma_start(out=a_bytes[0][:, 0:1, :], in_=av[0][:, 0:1, :])
-        nc.sync.dma_start(out=x_sb[0][:, 0:2, :], in_=xv[0][:, 0:2, :])
-        nc.sync.dma_start(out=x_sb[0][:, 2:4, :], in_=xv[0][:, 2:4, :])
-        nc.sync.dma_start(out=w_sb[:].bitcast(I32), in_=w_words[0].bitcast(I32))
-        nc.sync.dma_start(out=a_bytes[0][:, 1:2, :], in_=av[0][:, 1:2, :])
-        nc.sync.dma_start(out=x_sb[1][:], in_=xv[1])
-        nc.sync.dma_start(out=a_bytes[0][:, 2:4, :], in_=av[0][:, 2:4, :])
-        nc.sync.dma_start(out=a_bytes[1][:], in_=av[1])
-        nc.sync.dma_start(
-            out=mix_sb[:, 0:2, :].rearrange("p c f -> p (c f)"),
-            in_=mix[0:2, :].rearrange("c f -> (c f)").partition_broadcast(P),
-        )
-        nc.scalar.dma_start(out=mix_row[0:1, :], in_=mix[2:3, :])
-        nc.scalar.dma_start(out=a_scale[:], in_=adj_scale.rearrange("(g p t) j -> p g t j", p=P, t=T))
-        nc.scalar.dma_start(out=src_bf[:], in_=src_scale.rearrange("(g p t) -> p g t", p=P, t=T))
+        nc.vector.memset(w_scale_rows[:].bitcast(I32), 0)
+        nc.vector.memset(mix_row[:].bitcast(I32), 0)
+
+        x_view = x.rearrange("(g p t) k -> g p t k", p=P, t=PACK)
+        adj_view = adj_bytes.rearrange("(g p t) k -> g p t k", p=P, t=PACK)
+        nc.sync.dma_start(out=adj_codes[0][:, 0:1, :], in_=adj_view[0][:, 0:1, :])
+        for t0, t1 in ((0, 1), (1, 2), (2, 4)):
+            nc.sync.dma_start(out=x_rows[0][:, t0:t1, :], in_=x_view[0][:, t0:t1, :])
         for q in range(4):
-            nc.scalar.dma_start(
-                out=w_sc[32 * q : 32 * q + 4, :].bitcast(I32),
+            nc.sync.dma_start(
+                out=w_scale_rows[32 * q : 32 * q + 4, :].bitcast(I32),
                 in_=w_scales[0, 4 * q : 4 * q + 4, :].bitcast(I32),
             )
-
-        ident = keep.tile([P, P], F32, name="ident")
-        make_identity(nc, ident[:])
-        warm = keep.tile([P, 1], F32, name="warm")
-        nc.vector.memset(warm[:], 0.0)
-        warm2 = keep.tile([P, 1], F32, name="warm2")
-        nc.scalar.activation(out=warm2[:], in_=warm[:], func=ACT.Exp)
-        src = keep.tile([P, 2, G * T], F32, name="src")
-        nc.vector.tensor_copy(out=src[:, 0, :], in_=src_bf[:].rearrange("p g t -> p (g t)"))
-        nc.vector.tensor_scalar(
-            out=src[:, 1, :], in0=src_bf[:].rearrange("p g t -> p (g t)"), scalar1=-1.0, scalar2=None, op0=ALU.mult
+        nc.sync.dma_start(out=w_codes[:].bitcast(I32), in_=w_words[0].bitcast(I32))
+        nc.sync.dma_start(out=adj_codes[0][:, 1:2, :], in_=adj_view[0][:, 1:2, :])
+        nc.sync.dma_start(out=x_rows[1][:], in_=x_view[1])
+        nc.sync.dma_start(out=adj_codes[0][:, 2:4, :], in_=adj_view[0][:, 2:4, :])
+        nc.sync.dma_start(
+            out=mix_all[:, LOW:IDENTITY, :].rearrange("p c f -> p (c f)"),
+            in_=mix[LOW:IDENTITY, :].rearrange("c f -> (c f)").partition_broadcast(P),
         )
+        nc.sync.dma_start(out=adj_codes[1][:], in_=adj_view[1])
+        nc.scalar.dma_start(out=adj_factors[:], in_=adj_scale.rearrange("(g p t) j -> p g t j", p=P, t=PACK))
+        nc.scalar.dma_start(
+            out=factors_bf16[:].rearrange("p (g t) -> p g t", t=PACK),
+            in_=src_scale.rearrange("(g p t) -> p g t", p=P, t=PACK),
+        )
+        nc.scalar.dma_start(out=mix_row[0:1, :], in_=mix[IDENTITY : IDENTITY + 1, :])
 
-        xq, xs, xi = [], [], []
-        for g in range(G):
-            xi.append(keep.tile([P, T * P * 4], BF16, name="xi%d" % g, align_bytes=64))
-            xq.append(keep.tile([P, T * P], U32, name="xq%d" % g, align_bytes=64))
-            xs.append(keep.tile([P, T * P], U8, name="xs%d" % g, align_bytes=64))
-        raw, ti, tq, ts = {}, {}, {}, {}
-        for g in range(G):
-            for c in range(2):
-                raw[g, c] = keep.tile([P, T, F], BF16, name="raw%d%d" % (g, c), align_bytes=64)
-                ti[g, c] = keep.tile([P, F, T], BF16, name="ti%d%d" % (g, c), align_bytes=64)
-                tq[g, c] = keep.tile([P, F], U32, name="tq%d%d" % (g, c), align_bytes=64)
-                ts[g, c] = keep.tile([P, F], U8, name="ts%d%d" % (g, c), align_bytes=64)
-        aw, ai, aq, as_, score = [], [], [], [], []
-        for i in range(G * T):
-            aw.append(keep.tile([P, N], BF16, name="aw%d" % i, align_bytes=64))
-            ai.append(keep.tile([P, 2 * P * 4], BF16, name="ai%d" % i, align_bytes=64))
-            aq.append(keep.tile([P, 2 * P], U32, name="aq%d" % i, align_bytes=64))
-            as_.append(keep.tile([P, 2 * P], U8, name="as%d" % i, align_bytes=64))
+        factors = keep.tile([P, 2, TILES], F32, name="factors")
+        x_words, x_codes, x_scales = [], [], []
+        for g in range(GROUPS):
+            x_words.append(keep.tile([P, PACK * P * PACK], BF16, name="x_words%d" % g, align_bytes=64))
+            x_codes.append(keep.tile([P, PACK * P], U32, name="x_codes%d" % g, align_bytes=64))
+            x_scales.append(keep.tile([P, PACK * P], U8, name="x_scales%d" % g, align_bytes=64))
+        t_rows, t_words, t_codes, t_scales = {}, {}, {}, {}
+        for g in range(GROUPS):
+            for c in (LOW, HIGH):
+                t_rows[g, c] = keep.tile([P, PACK, F], BF16, name="t_rows%d%d" % (g, c), align_bytes=64)
+                t_words[g, c] = keep.tile([P, F, PACK], BF16, name="t_words%d%d" % (g, c), align_bytes=64)
+                t_codes[g, c] = keep.tile([P, F], U32, name="t_codes%d%d" % (g, c), align_bytes=64)
+                t_scales[g, c] = keep.tile([P, F], U8, name="t_scales%d%d" % (g, c), align_bytes=64)
+        adj_rows, adj_words, adj_mx, adj_mx_scales, score = [], [], [], [], []
+        for i in range(TILES):
+            adj_rows.append(keep.tile([P, N], BF16, name="adj_rows%d" % i, align_bytes=64))
+            adj_words.append(keep.tile([P, GROUPS * P * PACK], BF16, name="adj_words%d" % i, align_bytes=64))
+            adj_mx.append(keep.tile([P, GROUPS * P], U32, name="adj_mx%d" % i, align_bytes=64))
+            adj_mx_scales.append(keep.tile([P, GROUPS * P], U8, name="adj_mx_scales%d" % i, align_bytes=64))
             score.append(keep.tile([P, 5], F32, name="score%d" % i))
 
-        def bank_of(tag, bufs):
-            b = psum.tile([P, 512], F32, name="b_" + tag, tag=tag, bufs=bufs)
-            return b
+        spark = keep.tile([P, 2], F32, name="spark")
+        nc.vector.memset(spark[:, 0:1], 0.0)
+        nc.scalar.activation(out=spark[:, 1:2], in_=spark[:, 0:1], func=ACT.Exp)
 
-        def main():
-            return bank_of("main", 5)
+        def rotating_bank():
+            bank = psum.tile([P, BANK], F32, name="rotating", tag="rotating", bufs=5)
+            return bank
 
-        def spread_mix(c, copy):
-            bank = main()
-            nc.tensor.matmul(bank[:], lhsT=ones[:], rhs=mix_row[:], start=True, stop=True)
-            copy(out=mix_sb[:, c, :], in_=bank[:])
+        def identity_bank():
+            bank = psum.tile([P, BANK], F32, name="identity", tag="identity", bufs=2)
+            return bank
 
-        def turn_x(g, h, copy):
-            bank = main()
-            bv = bank[:].rearrange("p (j u r) -> p j u r", j=2, u=2)
-            for j in range(2):
-                words = x_sb[g][:, 2 * h + j, :].bitcast(F32)
+        def turning_bank():
+            bank = psum.tile([P, BANK], F32, name="turning", tag="turning", bufs=1)
+            return bank
+
+        def turn_x(first, count):
+            g, t = divmod(first, PACK)
+            bank = rotating_bank()
+            turned = bank[:, 0 : count * 2 * P].rearrange("p (j u r) -> p j u r", j=count, u=2)
+            for j in range(count):
+                words = x_rows[g][:, t + j, :].bitcast(F32)
                 for u in range(2):
-                    nc.tensor.transpose(bv[:, j, u, :], words[:, u : D // 2 : 2], ident[:])
-            xiw = xi[g][:].bitcast(F32).rearrange("p (t r u) -> p t r u", t=T, u=2)
-            copy(out=xiw[:, 2 * h : 2 * h + 2], in_=bv.rearrange("p j u r -> p j r u"))
+                    nc.tensor.transpose(turned[:, j, u, :], words[:, u : D // 2 : 2], eye[:])
+            by_row = x_words[g][:].bitcast(F32).rearrange("p (t r u) -> p t r u", t=PACK, u=2)
+            nc.scalar.copy(out=by_row[:, t : t + count], in_=turned.rearrange("p j u r -> p j r u"))
 
-        def quant_x(g, h):
-            cols = slice(2 * h * P, 2 * (h + 1) * P)
+        def quantise_x(first, count):
+            g, t = divmod(first, PACK)
+            rows = slice(t * P, (t + count) * P)
             nc.vector.quantize_mx(
-                out=xq[g][:, cols].bitcast(FP8X4), scales=xs[g][:, cols], in_=xi[g][:, 8 * h * P : 8 * (h + 1) * P]
+                out=x_codes[g][:, rows].bitcast(FP8X4),
+                scales=x_scales[g][:, rows],
+                in_=x_words[g][:, t * P * PACK : (t + count) * P * PACK],
             )
 
-        def project(bank, i, c, start, stop):
-            g, t = divmod(i, T)
+        def project(bank, i, channel, stop):
+            g, t = divmod(i, PACK)
+            nodes = slice(t * P, (t + 1) * P)
             nc.tensor.matmul_mx(
-                out=bank,
-                lhsT=xq[g][:, t * P : (t + 1) * P].bitcast(FP8X4),
-                lhsT_scale=xs[g][:, t * P : (t + 1) * P],
-                rhs=w_sb[:, 2 * F * c : 2 * F * (c + 1)].bitcast(FP4X4),
-                rhs_scale=w_sc[:, F * c : F * (c + 1)],
-                start=start,
+                out=bank[:],
+                lhsT=x_codes[g][:, nodes].bitcast(FP8X4),
+                lhsT_scale=x_scales[g][:, nodes],
+                rhs=w_codes[:, 2 * F * channel : 2 * F * (channel + 1)].bitcast(FP4X4),
+                rhs_scale=w_scale_rows[:, F * channel : F * (channel + 1)],
+                start=True,
                 stop=stop,
             )
 
-        def source(g, c, t, on_vector):
-            hb = main()
-            project(hb[:], g * T + t, c, True, True)
-            s = src[:, c, g * T + t : g * T + t + 1]
-            if on_vector:
-                nc.vector.tensor_scalar(out=raw[g, c][:, t, :], in0=hb[:], scalar1=s, scalar2=None, op0=ALU.mult)
-            else:
-                nc.scalar.activation(out=raw[g, c][:, t, :], in_=hb[:], func=ACT.Copy, scale=s)
+        def make_factors():
+            nc.vector.tensor_copy(out=factors[:, LOW, :], in_=factors_bf16[:])
+            nc.vector.tensor_scalar(
+                out=factors[:, HIGH, :], in0=factors_bf16[:], scalar1=-1.0, scalar2=None, op0=ALU.mult
+            )
 
-        def interleave(g, c):
+        def source(i, channel):
+            g, t = divmod(i, PACK)
+            bank = rotating_bank()
+            project(bank, i, channel, True)
+            nc.scalar.activation(
+                out=t_rows[g, channel][:, t, :], in_=bank[:], func=ACT.Copy, scale=factors[:, channel, i : i + 1]
+            )
+
+        def interleave_on_vector(g, channel):
             nc.vector.tensor_copy(
-                out=ti[g, c][:].rearrange("p (c i) t -> p c t i", i=4),
-                in_=raw[g, c][:].rearrange("p t (c i) -> p c t i", i=4),
+                out=t_words[g, channel][:].rearrange("p (c i) t -> p c t i", i=4),
+                in_=t_rows[g, channel][:].rearrange("p t (c i) -> p c t i", i=4),
             )
 
-        def interleave_gp(g, c):
+        def interleave_on_gpsimd(g, channel):
             nc.gpsimd.tensor_scalar(
-                out=ti[g, c][:], in0=raw[g, c][:].rearrange("p t f -> p f t"),
-                scalar1=1.0, scalar2=0.0, op0=ALU.mult, op1=ALU.add,
+                out=t_words[g, channel][:],
+                in0=t_rows[g, channel][:].rearrange("p t f -> p f t"),
+                scalar1=1.0,
+                scalar2=0.0,
+                op0=ALU.mult,
+                op1=ALU.add,
             )
 
-        def quant_t(g, c):
+        def quantise_t(g, channel):
             nc.vector.quantize_mx(
-                out=tq[g, c][:].bitcast(FP8X4), scales=ts[g, c][:], in_=ti[g, c][:].rearrange("p f t -> p (f t)")
+                out=t_codes[g, channel][:].bitcast(FP8X4),
+                scales=t_scales[g, channel][:],
+                in_=t_words[g, channel][:].rearrange("p f t -> p (f t)"),
             )
 
-        def widen(i, on_vector, j0=0, j1=NBLK):
-            g, t = divmod(i, T)
-            for j in range(j0, j1):
-                cols = slice(j * BLK, (j + 1) * BLK)
-                s = a_scale[:, g, t, j : j + 1]
-                src8 = a_bytes[g][:, t, cols].bitcast(FP8)
-                if on_vector:
-                    nc.vector.tensor_scalar(out=aw[i][:, cols], in0=src8, scalar1=s, scalar2=None, op0=ALU.mult)
-                else:
-                    nc.scalar.activation(out=aw[i][:, cols], in_=src8, func=ACT.Copy, scale=s)
+        def widen_on_vector(i, first, end):
+            g, t = divmod(i, PACK)
+            for j in range(first, end):
+                cols = slice(j * BLOCK, (j + 1) * BLOCK)
+                nc.vector.tensor_scalar(
+                    out=adj_rows[i][:, cols],
+                    in0=adj_codes[g][:, t, cols].bitcast(FP8),
+                    scalar1=adj_factors[:, g, t, j : j + 1],
+                    scalar2=None,
+                    op0=ALU.mult,
+                )
 
-        turned = {}
+        def widen_on_scalar(i, first, end):
+            g, t = divmod(i, PACK)
+            for j in range(first, end):
+                cols = slice(j * BLOCK, (j + 1) * BLOCK)
+                nc.scalar.activation(
+                    out=adj_rows[i][:, cols],
+                    in_=adj_codes[g][:, t, cols].bitcast(FP8),
+                    func=ACT.Copy,
+                    scale=adj_factors[:, g, t, j : j + 1],
+                )
 
-        def turn_a(i):
-            words = aw[i][:].bitcast(F32)
-            bank = bank_of("turn", 1)
-            bv = bank[:].rearrange("p (q u r) -> p q u r", q=2, u=2)
-            for q in range(2):
+        turned_adj = {}
+
+        def turn_adj(i):
+            words = adj_rows[i][:].bitcast(F32)
+            half = N // GROUPS // 2
+            bank = turning_bank()
+            turned_adj[i] = bank[:].rearrange("p (g u r) -> p g u r", g=GROUPS, u=2)
+            for g in range(GROUPS):
                 for u in range(2):
-                    nc.tensor.transpose(bv[:, q, u, :], words[:, 256 * q + u : 256 * (q + 1) : 2], ident[:])
-            turned[i] = bv
+                    nc.tensor.transpose(turned_adj[i][:, g, u, :], words[:, half * g + u : half * (g + 1) : 2], eye[:])
 
-        def take_a(i, copy):
-            copy(
-                out=ai[i][:].bitcast(F32).rearrange("p (q r u) -> p q r u", q=2, u=2),
-                in_=turned[i].rearrange("p q u r -> p q r u"),
+        def take_adj(i):
+            nc.scalar.copy(
+                out=adj_words[i][:].bitcast(F32).rearrange("p (g r u) -> p g r u", g=GROUPS, u=2),
+                in_=turned_adj[i].rearrange("p g u r -> p g r u"),
             )
 
-        def quant_a(i):
-            nc.vector.quantize_mx(out=aq[i][:].bitcast(FP8X4), scales=as_[i][:], in_=ai[i][:])
+        def quantise_adj(i):
+            nc.vector.quantize_mx(out=adj_mx[i][:].bitcast(FP8X4), scales=adj_mx_scales[i][:], in_=adj_words[i][:])
 
         banks = {}
 
-        def rate(i, c):
-            junk = work.tile([P, F], F32, name="junk")
+        def open_bank(i, channel):
+            banks[i, channel] = rotating_bank()
+
+        def propagate(i, channel):
+            bank = banks[i, channel]
+            if channel == HIGH:
+                project(bank, i, HIGH, False)
+            for g in range(GROUPS):
+                nodes = slice(g * P, (g + 1) * P)
+                nc.tensor.matmul_mx(
+                    out=bank[:],
+                    lhsT=adj_mx[i][:, nodes].bitcast(FP8X4),
+                    lhsT_scale=adj_mx_scales[i][:, nodes],
+                    rhs=t_codes[g, channel][:].bitcast(FP8X4),
+                    rhs_scale=t_scales[g, channel][:],
+                    start=(channel == LOW and g == 0),
+                    stop=(g == GROUPS - 1),
+                )
+
+        def propagate_new(i, channel):
+            open_bank(i, channel)
+            propagate(i, channel)
+
+        def identity_product(i, bank):
+            banks[i, IDENTITY] = bank
+            project(bank, i, IDENTITY, True)
+
+        def rate(i, channel):
+            products = work.tile([P, F], F32, name="products")
             nc.vector.scalar_tensor_tensor(
-                out=junk[:], in0=banks[i, c][:], scalar=0.0, in1=mix_sb[:, c, :], op0=ALU.max, op1=ALU.mult,
-                accum_out=score[i][:, c : c + 1],
+                out=products[:],
+                in0=banks[i, channel][:],
+                scalar=0.0,
+                in1=mix_all[:, channel, :],
+                op0=ALU.max,
+                op1=ALU.mult,
+                accum_out=score[i][:, channel : channel + 1],
             )
 
-        def identity_channel(i):
-            banks[i, 2] = bank_of("id", 2)
-            project(banks[i, 2][:], i, 2, True, True)
+        bias, e, total, inverse, alpha_high, weighted, y = {}, {}, {}, {}, {}, {}, {}
 
-        def propagate(i):
-            for c in range(2):
-                banks[i, c] = main()
-                pb = banks[i, c]
-                if c == 1:
-                    project(pb[:], i, 1, True, False)
-                for q in range(2):
-                    nc.tensor.matmul_mx(
-                        out=pb[:],
-                        lhsT=aq[i][:, q * P : (q + 1) * P].bitcast(FP8X4),
-                        lhsT_scale=as_[i][:, q * P : (q + 1) * P],
-                        rhs=tq[q, c][:].bitcast(FP8X4),
-                        rhs_scale=ts[q, c][:],
-                        start=(c == 0 and q == 0),
-                        stop=(q == 1),
-                    )
-
-        low, w, tot, inv, a1 = {}, {}, {}, {}, {}
-
-        def soft_o(i):
+        def lower_scores(i):
             nc.vector.tensor_scalar(
-                out=score[i][:, 3:5], in0=score[i][:, 0:2], scalar1=SPREAD, scalar2=None, op0=ALU.subtract
+                out=score[i][:, 3:5], in0=score[i][:, LOW:IDENTITY], scalar1=SPREAD, scalar2=None, op0=ALU.subtract
             )
 
-        def soft_m(i):
-            low[i] = work.tile([P, 1], F32, name="low")
-            nc.vector.tensor_reduce(out=low[i][:], in_=score[i][:, 2:5], axis=AX.X, op=ALU.max, negate=True)
+        def reference_score(i):
+            bias[i] = work.tile([P, 1], F32, name="bias")
+            nc.vector.tensor_reduce(
+                out=bias[i][:], in_=score[i][:, IDENTITY:5], axis=AX.X, op=ALU.max, negate=True
+            )
 
-        def soft_e(i):
-            w[i] = work.tile([P, 3], F32, name="w")
-            tot[i] = work.tile([P, 1], F32, name="tot")
+        def exponentials(i):
+            e[i] = work.tile([P, 3], F32, name="e")
+            total[i] = work.tile([P, 1], F32, name="total")
             nc.scalar.activation(
-                out=w[i][:], in_=score[i][:, 0:3], func=ACT.Exp, bias=low[i][:], accum_out=tot[i][:]
+                out=e[i][:], in_=score[i][:, LOW : IDENTITY + 1], func=ACT.Exp, bias=bias[i][:], accum_out=total[i][:]
             )
 
-        def soft_i(i):
-            inv[i] = work.tile([P, 1], F32, name="inv")
-            nc.vector.reciprocal(out=inv[i][:], in_=tot[i][:])
+        def invert_total(i):
+            inverse[i] = work.tile([P, 1], F32, name="inverse")
+            nc.vector.reciprocal(out=inverse[i][:], in_=total[i][:])
 
-        def soft_a(i):
-            a1[i] = work.tile([P, 1], F32, name="a1")
-            nc.scalar.activation(out=a1[i][:], in_=w[i][:, 1:2], func=ACT.Copy, scale=inv[i][:])
+        def high_share(i):
+            alpha_high[i] = work.tile([P, 1], F32, name="alpha_high")
+            nc.scalar.activation(
+                out=alpha_high[i][:], in_=e[i][:, HIGH : HIGH + 1], func=ACT.Copy, scale=inverse[i][:]
+            )
 
-        ov = out.rearrange("(g p t) f -> g t p f", p=P, t=T)
-        r, y = {}, {}
+        def weigh(i, channel, weight, cols=slice(0, F)):
+            if (i, channel) not in weighted:
+                weighted[i, channel] = work.tile([P, F], F32, name="weighted%d" % channel)
+            nc.scalar.activation(
+                out=weighted[i, channel][:, cols], in_=banks[i, channel][:, cols], func=ACT.Relu, scale=weight
+            )
 
-        def weigh(i, c, cols=slice(0, F)):
-            if cols.start == 0:
-                r[i, c] = work.tile([P, F], F32, name="r%d" % c)
-            s = w[i][:, 0:1] if c == 0 else a1[i][:]
-            nc.scalar.activation(out=r[i, c][:, cols], in_=banks[i, c][:, cols], func=ACT.Relu, scale=s)
+        def weigh_low(i, cols=slice(0, F)):
+            weigh(i, LOW, e[i][:, LOW : LOW + 1], cols)
 
-        o = {}
+        def weigh_high(i, cols=slice(0, F)):
+            weigh(i, HIGH, alpha_high[i][:], cols)
 
-        def add_a(i, cols=slice(0, F)):
-            if cols.start == 0:
+        def add_low(i, cols=slice(0, F)):
+            if i not in y:
                 y[i] = work.tile([P, F], F32, name="y")
             nc.vector.scalar_tensor_tensor(
-                out=y[i][:, cols], in0=banks[i, 2][:, cols], scalar=0.0, in1=r[i, 0][:, cols], op0=ALU.max, op1=ALU.add
+                out=y[i][:, cols],
+                in0=banks[i, IDENTITY][:, cols],
+                scalar=0.0,
+                in1=weighted[i, LOW][:, cols],
+                op0=ALU.max,
+                op1=ALU.add,
             )
 
-        def add_b(i, cols=slice(0, F)):
-            g, t = divmod(i, T)
-            if cols.start == 0:
-                o[i] = work.tile([P, F], F32, name="o")
+        out_view = out.rearrange("(g p t) f -> g t p f", p=P, t=PACK)
+        results = {}
+
+        def add_high(i, cols=slice(0, F)):
+            g, t = divmod(i, PACK)
+            if i not in results:
+                results[i] = work.tile([P, F], F32, name="result")
             nc.vector.scalar_tensor_tensor(
-                out=o[i][:, cols], in0=y[i][:, cols], scalar=inv[i][:], in1=r[i, 1][:, cols], op0=ALU.mult, op1=ALU.add
+                out=results[i][:, cols],
+                in0=y[i][:, cols],
+                scalar=inverse[i][:],
+                in1=weighted[i, HIGH][:, cols],
+                op0=ALU.mult,
+                op1=ALU.add,
             )
-            nc.sync.dma_start(out=ov[g, t][:, cols], in_=o[i][:, cols])
+            nc.sync.dma_start(out=out_view[g, t][:, cols], in_=results[i][:, cols])
 
-        sc, ve = nc.scalar.copy, nc.vector.tensor_copy
+        def spread_identity_mix():
+            bank = rotating_bank()
+            nc.tensor.matmul(bank[:], lhsT=ones[:], rhs=mix_row[:], start=True, stop=True)
+            nc.scalar.copy(out=mix_all[:, IDENTITY, :], in_=bank[:])
+
         with tc.manual_schedule():
-            spread_mix(2, sc)
-            turn_x(0, 0, sc)
-            widen(0, True)
-            quant_x(0, 0)
-            turn_x(0, 1, sc)
-            quant_x(0, 1)
-            for t in range(2):
-                source(0, 0, t, False)
-                identity_channel(t)
-                rate(t, 2)
-            turn_x(1, 0, sc)
-            turn_x(1, 1, sc)
-            quant_x(1, 0)
-            quant_x(1, 1)
-            for t in range(2, T):
-                source(0, 0, t, False)
-            for t in range(T):
-                source(0, 1, t, False)
-                if t < R3:
-                    identity_channel(2 + t)
-                    rate(2 + t, 2)
-            interleave(0, 0)
-            source(1, 0, 0, False)
-            identity_channel(2 + R3)
-            rate(2 + R3, 2)
-            quant_t(0, 0)
-            interleave(0, 1)
-            source(1, 0, 1, False)
-            identity_channel(3 + R3)
-            rate(3 + R3, 2)
-            for t in range(2, T):
-                source(1, 0, t, False)
-            quant_t(0, 1)
-            turn_a(0)
-            take_a(0, sc)
-            interleave(1, 0)
-            for t in range(T):
-                source(1, 1, t, t >= RAWV)
-            quant_a(0)
-            quant_t(1, 0)
-            for i in range(4 + R3, REST):
-                identity_channel(i)
-                rate(i, 2)
-            widen(1, False)
-            interleave(1, 1)
-            turn_a(1)
-            take_a(1, sc)
-            quant_a(1)
-            quant_t(1, 1)
-            propagate(0)
-            widen(2, False)
-            turn_a(2)
+            widen_on_vector(0, 0, BLOCKS)
+            for i in (0, 1):
+                turn_x(i, 1)
+                quantise_x(i, 1)
+            make_factors()
+            turn_x(2, 2)
+            spread_identity_mix()
+            quantise_x(2, 2)
+            widen_on_vector(1, 0, BLOCKS)
+            for i in (0, 1):
+                source(i, LOW)
+                identity_product(i, identity_bank())
+                rate(i, IDENTITY)
+            for i in (4, 6):
+                turn_x(i, 2)
+            for i in (4, 6):
+                quantise_x(i, 2)
+            for i in (2, 3):
+                source(i, LOW)
+            interleave_on_gpsimd(0, LOW)
+            for i in range(4):
+                source(i, HIGH)
+                identity_product(i + 2, turning_bank() if i == 1 else identity_bank())
+                rate(i + 2, IDENTITY)
+            for i in (4, 5):
+                source(i, LOW)
+                identity_product(i + 2, identity_bank())
+                rate(i + 2, IDENTITY)
+            quantise_t(0, LOW)
+            interleave_on_vector(0, HIGH)
+            turn_adj(0)
+            take_adj(0)
+            for i in (6, 7):
+                source(i, LOW)
+            quantise_adj(0)
+            quantise_t(0, HIGH)
+            interleave_on_vector(1, LOW)
+            for i in (4, 5):
+                source(i, HIGH)
+            turn_adj(1)
+            take_adj(1)
+            for i in (6, 7):
+                source(i, HIGH)
+            quantise_adj(1)
+            quantise_t(1, LOW)
+            widen_on_scalar(2, 0, BLOCKS)
+            interleave_on_vector(1, HIGH)
 
-            for s in range(NT):
+            propagate_new(0, LOW)
+            rate(0, LOW)
+            open_bank(0, HIGH)
+            propagate_new(1, LOW)
+            turn_adj(2)
+            take_adj(2)
+            quantise_t(1, HIGH)
+            rate(1, LOW)
+            propagate(0, HIGH)
+            propagate_new(1, HIGH)
+            widen_on_scalar(3, 0, BLOCKS)
+            turn_adj(3)
+            widen_on_scalar(4, VECTOR_BLOCKS, BLOCKS)
+            take_adj(3)
+
+            for s in range(TILES):
+                last = s - 1
+                more_adj = s + 3 < TILES
                 if s > 0:
-                    weigh(s - 1, 0)
-                    soft_a(s - 1)
-                    weigh(s - 1, 1)
-                if s + 2 < NT:
-                    take_a(s + 2, sc)
-                rate(s, 0)
-                rate(s, 1)
-                if s == NT - 1:
-                    soft_o(s)
-                    soft_m(s)
+                    weigh_low(last)
+                if s > 0 and not more_adj:
+                    invert_total(last)
+                rate(s, HIGH)
+                if s > 0 and more_adj:
+                    invert_total(last)
                 if s > 0:
-                    identity_channel(s - 1)
-                    add_a(s - 1)
-                if s < NT - 1:
-                    soft_o(s)
+                    high_share(last)
+                    weigh_high(last)
+                if s > 0 and more_adj:
+                    take_adj(s + 3)
+                if s + 2 < TILES:
+                    quantise_adj(s + 2)
+                if 0 < s < TILES - 1:
+                    rate(s + 1, LOW)
+                lower_scores(s)
                 if s > 0:
-                    add_b(s - 1)
-                if s < NT - 1:
-                    soft_m(s)
-                if s + 1 < NT:
-                    propagate(s + 1)
-                if s + AHEAD < NT:
-                    identity_channel(s + AHEAD)
-                    rate(s + AHEAD, 2)
-                if s + 3 < NT:
-                    widen(s + 3, True, 0, VB)
-                    widen(s + 3, False, VB, NBLK)
-                if s + 2 < NT:
-                    quant_a(s + 2)
-                soft_e(s)
-                if s + 3 < NT:
-                    turn_a(s + 3)
-                soft_i(s)
-            i = NT - 1
-            identity_channel(i)
-            halves = (slice(0, F // 2), slice(F // 2, F))
-            for cols in halves:
-                weigh(i, 0, cols)
-                add_a(i, cols)
-            soft_a(i)
-            for cols in halves:
-                weigh(i, 1, cols)
-                add_b(i, cols)
+                    identity_product(last, identity_bank())
+                    add_low(last)
+                if 0 < s < TILES - 1:
+                    propagate_new(s + 1, HIGH)
+                reference_score(s)
+                if s + 4 < TILES:
+                    widen_on_vector(s + 4, 0, VECTOR_BLOCKS)
+                if s > 0:
+                    add_high(last)
+                if 0 < s and s + 4 < TILES:
+                    widen_on_scalar(s + 4, VECTOR_BLOCKS, BLOCKS)
+                exponentials(s)
+                if s + 2 < TILES:
+                    propagate_new(s + 2, LOW)
+                if s + 4 < TILES:
+                    turn_adj(s + 4)
+
+            last = TILES - 1
+            left, right = slice(0, F // 2), slice(F // 2, F)
+            identity_product(last, identity_bank())
+            weigh_low(last, left)
+            invert_total(last)
+            add_low(last, left)
+            weigh_low(last, right)
+            add_low(last, right)
+            high_share(last)
+            for cols in (left, right):
+                weigh_high(last, cols)
+                add_high(last, cols)

from contextlib import ExitStack

import concourse.mybir as mybir
from concourse.masks import make_identity

N, D, F = 1024, 512, 512
FLOPS = 2 * N * D * 3 * F + 2 * N * N * 2 * F

F32 = mybir.dt.float32
BF16 = mybir.dt.bfloat16
U32 = mybir.dt.uint32
I32 = mybir.dt.int32
U8 = mybir.dt.uint8
FP8 = mybir.dt.float8_e4m3fn
FP8X4 = mybir.dt.float8_e4m3fn_x4
FP4X4 = mybir.dt.float4_e2m1fn_x4
ACT = mybir.ActivationFunctionType
ALU = mybir.AluOpType
AX = mybir.AxisListType

P = 128
PACK = 4
GROUPS = N // (P * PACK)
TILES = GROUPS * PACK
BANK = 512
BLOCK = 128
BLOCKS = N // BLOCK
LOW, HIGH, IDENTITY = 0, 1, 2

SPREAD = 46.0
VECTOR_BLOCKS = 3


def tile_acmgnnthreefilterchannelmixing_d1p_kernel(
    tc, x, w_words, w_scales, adj_bytes, adj_scale, src_scale, mix, out
):
    nc = tc.nc
    with ExitStack() as ctx:
        keep = ctx.enter_context(tc.tile_pool(name="keep", bufs=1))
        work = ctx.enter_context(tc.tile_pool(name="work", bufs=3))
        psum = ctx.enter_context(tc.psum_pool(name="psum", bufs=1))

        x_rows = [keep.tile([P, PACK, D], BF16, name="x_rows%d" % g, align_bytes=64) for g in range(GROUPS)]
        adj_codes = [keep.tile([P, PACK, N], U8, name="adj_codes%d" % g, align_bytes=64) for g in range(GROUPS)]
        adj_factors = keep.tile([P, GROUPS, PACK, BLOCKS], F32, name="adj_factors")
        w_codes = keep.tile([P, 2 * 3 * F], U8, name="w_codes", align_bytes=64)
        w_scale_rows = keep.tile([P, 3 * F], U8, name="w_scale_rows", align_bytes=64)
        factors_bf16 = keep.tile([P, TILES], BF16, name="factors_bf16")
        mix_row = keep.tile([P, F], BF16, name="mix_row", align_bytes=64)
        mix_all = keep.tile([P, 3, F], BF16, name="mix_all", align_bytes=64)

        eye = keep.tile([P, P], F32, name="eye")
        make_identity(nc, eye[:])
        ones = keep.tile([P, P], BF16, name="ones", align_bytes=64)
        nc.gpsimd.memset(ones[:], 1.0)
        nc.vector.memset(w_scale_rows[:].bitcast(I32), 0)
        nc.vector.memset(mix_row[:].bitcast(I32), 0)

        x_view = x.rearrange("(g p t) k -> g p t k", p=P, t=PACK)
        adj_view = adj_bytes.rearrange("(g p t) k -> g p t k", p=P, t=PACK)
        nc.sync.dma_start(out=adj_codes[0][:, 0:1, :], in_=adj_view[0][:, 0:1, :])
        for t0, t1 in ((0, 1), (1, 2), (2, 4)):
            nc.sync.dma_start(out=x_rows[0][:, t0:t1, :], in_=x_view[0][:, t0:t1, :])
        for q in range(4):
            nc.sync.dma_start(
                out=w_scale_rows[32 * q : 32 * q + 4, :].bitcast(I32),
                in_=w_scales[0, 4 * q : 4 * q + 4, :].bitcast(I32),
            )
        nc.sync.dma_start(out=w_codes[:].bitcast(I32), in_=w_words[0].bitcast(I32))
        nc.sync.dma_start(out=adj_codes[0][:, 1:2, :], in_=adj_view[0][:, 1:2, :])
        nc.sync.dma_start(out=x_rows[1][:], in_=x_view[1])
        nc.sync.dma_start(out=adj_codes[0][:, 2:4, :], in_=adj_view[0][:, 2:4, :])
        nc.sync.dma_start(
            out=mix_all[:, LOW:IDENTITY, :].rearrange("p c f -> p (c f)"),
            in_=mix[LOW:IDENTITY, :].rearrange("c f -> (c f)").partition_broadcast(P),
        )
        nc.sync.dma_start(out=adj_codes[1][:], in_=adj_view[1])
        nc.scalar.dma_start(out=adj_factors[:], in_=adj_scale.rearrange("(g p t) j -> p g t j", p=P, t=PACK))
        nc.scalar.dma_start(
            out=factors_bf16[:].rearrange("p (g t) -> p g t", t=PACK),
            in_=src_scale.rearrange("(g p t) -> p g t", p=P, t=PACK),
        )
        nc.scalar.dma_start(out=mix_row[0:1, :], in_=mix[IDENTITY : IDENTITY + 1, :])

        factors = keep.tile([P, 2, TILES], F32, name="factors")
        x_words, x_codes, x_scales = [], [], []
        for g in range(GROUPS):
            x_words.append(keep.tile([P, PACK * P * PACK], BF16, name="x_words%d" % g, align_bytes=64))
            x_codes.append(keep.tile([P, PACK * P], U32, name="x_codes%d" % g, align_bytes=64))
            x_scales.append(keep.tile([P, PACK * P], U8, name="x_scales%d" % g, align_bytes=64))
        t_rows, t_words, t_codes, t_scales = {}, {}, {}, {}
        for g in range(GROUPS):
            for c in (LOW, HIGH):
                t_rows[g, c] = keep.tile([P, PACK, F], BF16, name="t_rows%d%d" % (g, c), align_bytes=64)
                t_words[g, c] = keep.tile([P, F, PACK], BF16, name="t_words%d%d" % (g, c), align_bytes=64)
                t_codes[g, c] = keep.tile([P, F], U32, name="t_codes%d%d" % (g, c), align_bytes=64)
                t_scales[g, c] = keep.tile([P, F], U8, name="t_scales%d%d" % (g, c), align_bytes=64)
        adj_rows, adj_words, adj_mx, adj_mx_scales, score = [], [], [], [], []
        for i in range(TILES):
            adj_rows.append(keep.tile([P, N], BF16, name="adj_rows%d" % i, align_bytes=64))
            adj_words.append(keep.tile([P, GROUPS * P * PACK], BF16, name="adj_words%d" % i, align_bytes=64))
            adj_mx.append(keep.tile([P, GROUPS * P], U32, name="adj_mx%d" % i, align_bytes=64))
            adj_mx_scales.append(keep.tile([P, GROUPS * P], U8, name="adj_mx_scales%d" % i, align_bytes=64))
            score.append(keep.tile([P, 5], F32, name="score%d" % i))

        spark = keep.tile([P, 2], F32, name="spark")
        nc.vector.memset(spark[:, 0:1], 0.0)
        nc.scalar.activation(out=spark[:, 1:2], in_=spark[:, 0:1], func=ACT.Exp)

        def rotating_bank():
            bank = psum.tile([P, BANK], F32, name="rotating", tag="rotating", bufs=5)
            return bank

        def identity_bank():
            bank = psum.tile([P, BANK], F32, name="identity", tag="identity", bufs=2)
            return bank

        def turning_bank():
            bank = psum.tile([P, BANK], F32, name="turning", tag="turning", bufs=1)
            return bank

        def turn_x(first, count):
            g, t = divmod(first, PACK)
            bank = rotating_bank()
            turned = bank[:, 0 : count * 2 * P].rearrange("p (j u r) -> p j u r", j=count, u=2)
            for j in range(count):
                words = x_rows[g][:, t + j, :].bitcast(F32)
                for u in range(2):
                    nc.tensor.transpose(turned[:, j, u, :], words[:, u : D // 2 : 2], eye[:])
            by_row = x_words[g][:].bitcast(F32).rearrange("p (t r u) -> p t r u", t=PACK, u=2)
            nc.scalar.copy(out=by_row[:, t : t + count], in_=turned.rearrange("p j u r -> p j r u"))

        def quantise_x(first, count):
            g, t = divmod(first, PACK)
            rows = slice(t * P, (t + count) * P)
            nc.vector.quantize_mx(
                out=x_codes[g][:, rows].bitcast(FP8X4),
                scales=x_scales[g][:, rows],
                in_=x_words[g][:, t * P * PACK : (t + count) * P * PACK],
            )

        def project(bank, i, channel, stop):
            g, t = divmod(i, PACK)
            nodes = slice(t * P, (t + 1) * P)
            nc.tensor.matmul_mx(
                out=bank[:],
                lhsT=x_codes[g][:, nodes].bitcast(FP8X4),
                lhsT_scale=x_scales[g][:, nodes],
                rhs=w_codes[:, 2 * F * channel : 2 * F * (channel + 1)].bitcast(FP4X4),
                rhs_scale=w_scale_rows[:, F * channel : F * (channel + 1)],
                start=True,
                stop=stop,
            )

        def make_factors():
            nc.vector.tensor_copy(out=factors[:, LOW, :], in_=factors_bf16[:])
            nc.vector.tensor_scalar(
                out=factors[:, HIGH, :], in0=factors_bf16[:], scalar1=-1.0, scalar2=None, op0=ALU.mult
            )

        def source(i, channel):
            g, t = divmod(i, PACK)
            bank = rotating_bank()
            project(bank, i, channel, True)
            nc.scalar.activation(
                out=t_rows[g, channel][:, t, :], in_=bank[:], func=ACT.Copy, scale=factors[:, channel, i : i + 1]
            )

        def interleave_on_vector(g, channel):
            nc.vector.tensor_copy(
                out=t_words[g, channel][:].rearrange("p (c i) t -> p c t i", i=4),
                in_=t_rows[g, channel][:].rearrange("p t (c i) -> p c t i", i=4),
            )

        def interleave_on_gpsimd(g, channel):
            nc.gpsimd.tensor_scalar(
                out=t_words[g, channel][:],
                in0=t_rows[g, channel][:].rearrange("p t f -> p f t"),
                scalar1=1.0,
                scalar2=0.0,
                op0=ALU.mult,
                op1=ALU.add,
            )

        def quantise_t(g, channel):
            nc.vector.quantize_mx(
                out=t_codes[g, channel][:].bitcast(FP8X4),
                scales=t_scales[g, channel][:],
                in_=t_words[g, channel][:].rearrange("p f t -> p (f t)"),
            )

        def widen_on_vector(i, first, end):
            g, t = divmod(i, PACK)
            for j in range(first, end):
                cols = slice(j * BLOCK, (j + 1) * BLOCK)
                nc.vector.tensor_scalar(
                    out=adj_rows[i][:, cols],
                    in0=adj_codes[g][:, t, cols].bitcast(FP8),
                    scalar1=adj_factors[:, g, t, j : j + 1],
                    scalar2=None,
                    op0=ALU.mult,
                )

        def widen_on_scalar(i, first, end):
            g, t = divmod(i, PACK)
            for j in range(first, end):
                cols = slice(j * BLOCK, (j + 1) * BLOCK)
                nc.scalar.activation(
                    out=adj_rows[i][:, cols],
                    in_=adj_codes[g][:, t, cols].bitcast(FP8),
                    func=ACT.Copy,
                    scale=adj_factors[:, g, t, j : j + 1],
                )

        turned_adj = {}

        def turn_adj(i):
            words = adj_rows[i][:].bitcast(F32)
            half = N // GROUPS // 2
            bank = turning_bank()
            turned_adj[i] = bank[:].rearrange("p (g u r) -> p g u r", g=GROUPS, u=2)
            for g in range(GROUPS):
                for u in range(2):
                    nc.tensor.transpose(turned_adj[i][:, g, u, :], words[:, half * g + u : half * (g + 1) : 2], eye[:])

        def take_adj(i):
            nc.scalar.copy(
                out=adj_words[i][:].bitcast(F32).rearrange("p (g r u) -> p g r u", g=GROUPS, u=2),
                in_=turned_adj[i].rearrange("p g u r -> p g r u"),
            )

        def quantise_adj(i):
            nc.vector.quantize_mx(out=adj_mx[i][:].bitcast(FP8X4), scales=adj_mx_scales[i][:], in_=adj_words[i][:])

        banks = {}

        def open_bank(i, channel):
            banks[i, channel] = rotating_bank()

        def propagate(i, channel):
            bank = banks[i, channel]
            if channel == HIGH:
                project(bank, i, HIGH, False)
            for g in range(GROUPS):
                nodes = slice(g * P, (g + 1) * P)
                nc.tensor.matmul_mx(
                    out=bank[:],
                    lhsT=adj_mx[i][:, nodes].bitcast(FP8X4),
                    lhsT_scale=adj_mx_scales[i][:, nodes],
                    rhs=t_codes[g, channel][:].bitcast(FP8X4),
                    rhs_scale=t_scales[g, channel][:],
                    start=(channel == LOW and g == 0),
                    stop=(g == GROUPS - 1),
                )

        def propagate_new(i, channel):
            open_bank(i, channel)
            propagate(i, channel)

        def identity_product(i, bank):
            banks[i, IDENTITY] = bank
            project(bank, i, IDENTITY, True)

        def rate(i, channel):
            products = work.tile([P, F], F32, name="products")
            nc.vector.scalar_tensor_tensor(
                out=products[:],
                in0=banks[i, channel][:],
                scalar=0.0,
                in1=mix_all[:, channel, :],
                op0=ALU.max,
                op1=ALU.mult,
                accum_out=score[i][:, channel : channel + 1],
            )

        bias, e, total, inverse, alpha_high, weighted, y = {}, {}, {}, {}, {}, {}, {}

        def lower_scores(i):
            nc.vector.tensor_scalar(
                out=score[i][:, 3:5], in0=score[i][:, LOW:IDENTITY], scalar1=SPREAD, scalar2=None, op0=ALU.subtract
            )

        def reference_score(i):
            bias[i] = work.tile([P, 1], F32, name="bias")
            nc.vector.tensor_reduce(
                out=bias[i][:], in_=score[i][:, IDENTITY:5], axis=AX.X, op=ALU.max, negate=True
            )

        def exponentials(i):
            e[i] = work.tile([P, 3], F32, name="e")
            total[i] = work.tile([P, 1], F32, name="total")
            nc.scalar.activation(
                out=e[i][:], in_=score[i][:, LOW : IDENTITY + 1], func=ACT.Exp, bias=bias[i][:], accum_out=total[i][:]
            )

        def invert_total(i):
            inverse[i] = work.tile([P, 1], F32, name="inverse")
            nc.vector.reciprocal(out=inverse[i][:], in_=total[i][:])

        def high_share(i):
            alpha_high[i] = work.tile([P, 1], F32, name="alpha_high")
            nc.scalar.activation(
                out=alpha_high[i][:], in_=e[i][:, HIGH : HIGH + 1], func=ACT.Copy, scale=inverse[i][:]
            )

        def weigh(i, channel, weight, cols=slice(0, F)):
            if (i, channel) not in weighted:
                weighted[i, channel] = work.tile([P, F], F32, name="weighted%d" % channel)
            nc.scalar.activation(
                out=weighted[i, channel][:, cols], in_=banks[i, channel][:, cols], func=ACT.Relu, scale=weight
            )

        def weigh_low(i, cols=slice(0, F)):
            weigh(i, LOW, e[i][:, LOW : LOW + 1], cols)

        def weigh_high(i, cols=slice(0, F)):
            weigh(i, HIGH, alpha_high[i][:], cols)

        def add_low(i, cols=slice(0, F)):
            if i not in y:
                y[i] = work.tile([P, F], F32, name="y")
            nc.vector.scalar_tensor_tensor(
                out=y[i][:, cols],
                in0=banks[i, IDENTITY][:, cols],
                scalar=0.0,
                in1=weighted[i, LOW][:, cols],
                op0=ALU.max,
                op1=ALU.add,
            )

        out_view = out.rearrange("(g p t) f -> g t p f", p=P, t=PACK)
        results = {}

        def add_high(i, cols=slice(0, F)):
            g, t = divmod(i, PACK)
            if i not in results:
                results[i] = work.tile([P, F], F32, name="result")
            nc.vector.scalar_tensor_tensor(
                out=results[i][:, cols],
                in0=y[i][:, cols],
                scalar=inverse[i][:],
                in1=weighted[i, HIGH][:, cols],
                op0=ALU.mult,
                op1=ALU.add,
            )
            nc.sync.dma_start(out=out_view[g, t][:, cols], in_=results[i][:, cols])

        def spread_identity_mix():
            bank = rotating_bank()
            nc.tensor.matmul(bank[:], lhsT=ones[:], rhs=mix_row[:], start=True, stop=True)
            nc.scalar.copy(out=mix_all[:, IDENTITY, :], in_=bank[:])

        with tc.manual_schedule():
            widen_on_vector(0, 0, BLOCKS)
            for i in (0, 1):
                turn_x(i, 1)
                quantise_x(i, 1)
            make_factors()
            turn_x(2, 2)
            spread_identity_mix()
            quantise_x(2, 2)
            widen_on_vector(1, 0, BLOCKS)
            for i in (0, 1):
                source(i, LOW)
                identity_product(i, identity_bank())
                rate(i, IDENTITY)
            for i in (4, 6):
                turn_x(i, 2)
            for i in (4, 6):
                quantise_x(i, 2)
            for i in (2, 3):
                source(i, LOW)
            interleave_on_gpsimd(0, LOW)
            for i in range(4):
                source(i, HIGH)
                identity_product(i + 2, turning_bank() if i == 1 else identity_bank())
                rate(i + 2, IDENTITY)
            for i in (4, 5):
                source(i, LOW)
                identity_product(i + 2, identity_bank())
                rate(i + 2, IDENTITY)
            quantise_t(0, LOW)
            interleave_on_vector(0, HIGH)
            turn_adj(0)
            take_adj(0)
            for i in (6, 7):
                source(i, LOW)
            quantise_adj(0)
            quantise_t(0, HIGH)
            interleave_on_vector(1, LOW)
            for i in (4, 5):
                source(i, HIGH)
            turn_adj(1)
            take_adj(1)
            for i in (6, 7):
                source(i, HIGH)
            quantise_adj(1)
            quantise_t(1, LOW)
            widen_on_scalar(2, 0, BLOCKS)
            interleave_on_vector(1, HIGH)

            propagate_new(0, LOW)
            rate(0, LOW)
            open_bank(0, HIGH)
            propagate_new(1, LOW)
            turn_adj(2)
            take_adj(2)
            quantise_t(1, HIGH)
            rate(1, LOW)
            propagate(0, HIGH)
            propagate_new(1, HIGH)
            widen_on_scalar(3, 0, BLOCKS)
            turn_adj(3)
            widen_on_scalar(4, VECTOR_BLOCKS, BLOCKS)
            take_adj(3)

            for s in range(TILES):
                last = s - 1
                more_adj = s + 3 < TILES
                if s > 0:
                    weigh_low(last)
                if s > 0 and not more_adj:
                    invert_total(last)
                rate(s, HIGH)
                if s > 0 and more_adj:
                    invert_total(last)
                if s > 0:
                    high_share(last)
                    weigh_high(last)
                if s > 0 and more_adj:
                    take_adj(s + 3)
                if s + 2 < TILES:
                    quantise_adj(s + 2)
                if 0 < s < TILES - 1:
                    rate(s + 1, LOW)
                lower_scores(s)
                if s > 0:
                    identity_product(last, identity_bank())
                    add_low(last)
                if 0 < s < TILES - 1:
                    propagate_new(s + 1, HIGH)
                reference_score(s)
                if s + 4 < TILES:
                    widen_on_vector(s + 4, 0, VECTOR_BLOCKS)
                if s > 0:
                    add_high(last)
                if 0 < s and s + 4 < TILES:
                    widen_on_scalar(s + 4, VECTOR_BLOCKS, BLOCKS)
                exponentials(s)
                if s + 2 < TILES:
                    propagate_new(s + 2, LOW)
                if s + 4 < TILES:
                    turn_adj(s + 4)

            last = TILES - 1
            left, right = slice(0, F // 2), slice(F // 2, F)
            identity_product(last, identity_bank())
            weigh_low(last, left)
            invert_total(last)
            add_low(last, left)
            weigh_low(last, right)
            add_low(last, right)
            high_share(last)
            for cols in (left, right):
                weigh_high(last, cols)
                add_high(last, cols)
